import numpy as np
import ml_dtypes


def mxq(x, axis, fmt="e4m3"):
    dtype, down = {"e4m3": (ml_dtypes.float8_e4m3fn, 7), "e5m2": (ml_dtypes.float8_e5m2, 14)}[fmt]
    v = np.moveaxis(np.asarray(x, np.float32).astype(ml_dtypes.bfloat16).astype(np.float64), axis, -1)
    blocks = v.reshape(v.shape[:-1] + (-1, 32))
    amax = np.abs(blocks).max(-1, keepdims=True)
    byte = np.maximum(np.where(amax > 0, np.frexp(amax)[1] - 1 + 127, 0) - down, 1)
    scale = np.exp2(byte - 127.0)
    codes = (blocks / scale).astype(np.float32).astype(dtype).astype(np.float64)
    return np.moveaxis((codes * scale).reshape(v.shape), -1, axis)


WIDE = False


def mx_kscale(k):
    if not WIDE:
        return np.ones(k)
    levels = np.array([10, -10, 5, -5, 0])
    if k % 512:
        return np.exp2(np.random.permutation(np.resize(levels, k // 32))).repeat(32)
    a = np.empty((k // 512, 16))
    for p in range(k // 512):
        a[p, :8] = np.random.permutation(np.resize(levels, 8))
        for g in range(8):
            far = levels[np.abs(levels - a[p, g]) >= 10]
            a[p, g + 8] = far[np.random.randint(len(far))]
    return np.exp2(a.ravel()).repeat(32)


def f64(x):
    return np.asarray(x).astype(np.float64)


def striped(idx):
    return np.tile(idx.reshape(-1, 16).T, (8, 1)).astype(np.uint16)


def unstriped(offs):
    return offs[:16].T.reshape(-1).astype(np.int64)


E2M1 = np.array([0.0, 0.5, 1.0, 1.5, 2.0, 3.0, 4.0, 6.0, -0.0, -0.5, -1.0, -1.5, -2.0, -3.0, -4.0, -6.0])


def pack_fp4(w):
    k, n = w.shape
    w = f64(np.asarray(w, np.float32).astype(ml_dtypes.bfloat16)).reshape(k // 32, 32, n)
    amax = np.abs(w).max(1)
    mant, ex = np.frexp(amax / 6.0)
    byte = np.clip(np.where(amax > 0, np.where(mant > 0.5, ex, ex - 1) + 127, 1), 1, 254)
    scaled = (w * np.exp2(127.0 - byte)[:, None, :]).reshape(k, n).astype(np.float32)
    c = np.ascontiguousarray(scaled.reshape(k // 512, 128, 4, n).transpose(0, 1, 3, 2)).astype(ml_dtypes.float4_e2m1fn).view(np.uint8) & 0xF
    words = (c[..., 0::2] | (c[..., 1::2] << 4)).reshape(k // 512, 128, 2 * n)
    return np.ascontiguousarray(words), np.ascontiguousarray(byte.astype(np.uint8).reshape(k // 512, 16, n))


def unpack_fp4(words, scales):
    g, _, n = scales.shape
    words = np.ascontiguousarray(words).reshape(g, 128, n, 2)
    nib = np.empty((g, 128, n, 4), np.uint8)
    nib[..., 0::2] = words & 0xF
    nib[..., 1::2] = words >> 4
    vals = E2M1[nib] * np.repeat(np.exp2(scales.astype(np.float64) - 127.0), 8, axis=1)[..., None]
    return vals.transpose(0, 1, 3, 2).reshape(g * 512, n)


K, T, S, D, H, N = 1024, 1024, 512, 2, 512, 128


def setup_inputs():
    n = np.random.standard_normal
    s = mx_kscale(K)[:, None]
    u = mx_kscale(H)
    packed_w2 = pack_fp4(n((H, N)) / np.sqrt(H) / u[:, None])
    return {
        "xT": (n((K, T)) * s).astype(np.float32),
        "w1": (n((K, H)) / np.sqrt(K) / s * u).astype(np.float32),
        "w2_words": packed_w2[0],
        "w2_scales": packed_w2[1],
        "taps": (n((H, D)) / np.sqrt(D)).astype(np.float32),
        "offs": striped(np.random.permutation(T)[:S]),
    }


def reference(xT, w1, w2_words, w2_scales, taps, offs):
    xq = mxq(f64(xT)[:, unstriped(offs)], 0, "e4m3")
    h = mxq(f64(w1), 0, "e4m3").T @ xq
    z = f64(taps)[:, 0:1] * h + f64(taps)[:, 1:2] * (np.pad(h, ((0, 0), (1, 0)))[:, :S])
    return unpack_fp4(w2_words, w2_scales).T @ mxq(z, 0, "e4m3")

@@ -1,0 +1,201 @@
+from contextlib import ExitStack
+
+import concourse.mybir as mybir
+
+K, T, S, H, N = 1024, 1024, 512, 512, 128
+FLOPS = 2 * K * H * S + 2 * H * N * S
+
+F32 = mybir.dt.float32
+BF16 = mybir.dt.bfloat16
+I32 = mybir.dt.int32
+U32 = mybir.dt.uint32
+U16 = mybir.dt.uint16
+U8 = mybir.dt.uint8
+FP8X4 = mybir.dt.float8_e4m3fn_x4
+FP4X4 = mybir.dt.float4_e2m1fn_x4
+COPY = mybir.ActivationFunctionType.Copy
+MULT = mybir.AluOpType.mult
+ADD = mybir.AluOpType.add
+
+P = 128
+PACK = 4
+K_PASS = P * PACK
+PASSES = K // K_PASS
+HALF = S // 2
+
+
+def tile_picked_dconv_none_e_kernel(tc, xT, w1, w2_words, w2_scales, taps, offs, out):
+    nc = tc.nc
+
+    def scalar_copy(dst, src):
+        nc.scalar.activation(out=dst, in_=src, func=COPY)
+
+    def vector_copy(dst, src):
+        nc.vector.tensor_copy(out=dst, in_=src)
+
+    with ExitStack() as ctx:
+        keep = ctx.enter_context(tc.tile_pool(name="keep", bufs=1))
+        psum = ctx.enter_context(tc.psum_pool(name="psum", bufs=1))
+
+        offsets = keep.tile([P, S // 16], U16, name="offsets")
+        w2_codes = keep.tile([P, 2 * N], U8, name="w2_codes", align_bytes=64)
+        w2_plane = keep.tile([P, N], U8, name="w2_plane", align_bytes=64)
+        tap = keep.tile([P, PACK, 2], F32, name="tap")
+        delayed = keep.tile([P, PACK, S + 8], F32, name="delayed")
+
+        nc.vector.memset(w2_plane[:].bitcast(I32), 0)
+        nc.vector.memset(delayed[:, :, 0:1], 0.0)
+
+        x_pieces = []
+        for c in range(PASSES):
+            rows = xT[c * K_PASS : (c + 1) * K_PASS, :].rearrange("(p u e) n -> p u e n", u=2, e=2)
+            for u in range(2):
+                for lo, hi in ((0, T // 2), (T // 2, T)):
+                    raw = keep.tile([P, 2, hi - lo], F32, name="x_raw_%d_%d_%d" % (c, u, lo))
+                    nc.sync.dma_start(out=raw[:], in_=rows[:, u, :, lo:hi])
+                    x_pieces.append((c, u, lo, hi, raw))
+                if c == 0 and u == 0:
+                    nc.sync.dma_start(offsets[:], offs)
+        w_raw = {}
+        for c in range(PASSES):
+            rows = w1[c * K_PASS : (c + 1) * K_PASS, :].rearrange("(p j) n -> p j n", j=PACK)
+            if c == PASSES - 1:
+                nc.sync.dma_start(out=tap[:], in_=taps.rearrange("(p t) d -> p t d", t=PACK))
+            for g in (1, 0):
+                w_raw[c, g] = keep.tile([P, PACK, H // 2], F32, name="w_raw_%d_%d" % (c, g))
+                nc.sync.dma_start(out=w_raw[c, g][:], in_=rows[:, :, g * (H // 2) : (g + 1) * (H // 2)])
+        nc.sync.dma_start(out=w2_codes[:].bitcast(I32), in_=w2_words[0].bitcast(I32))
+        for q in range(4):
+            nc.sync.dma_start(
+                out=w2_plane[32 * q : 32 * q + 4, :].bitcast(I32), in_=w2_scales[0, 4 * q : 4 * q + 4, :].bitcast(I32)
+            )
+
+        pairs = {(c, u): keep.tile([P, T], U32, name="pairs_%d_%d" % (c, u)) for c in range(PASSES) for u in range(2)}
+        picked = [keep.tile([P, 2, S], U32, name="picked_%d" % c) for c in range(PASSES)]
+        x_bf = [keep.tile([P, S * PACK], BF16, name="x_bf_%d" % c, align_bytes=64) for c in range(PASSES)]
+        x_codes = [keep.tile([P, S], U32, name="x_codes_%d" % c, align_bytes=64) for c in range(PASSES)]
+        x_plane = [keep.tile([P, S], U8, name="x_plane_%d" % c, align_bytes=64) for c in range(PASSES)]
+        w_both = keep.tile([P, 2 * PACK * H - H // 2], BF16, name="w_both", align_bytes=64)
+        w_bf = [
+            w_both[:, start : start + PACK * H].rearrange("p (t m j) -> p t m j", t=PACK, j=PACK)
+            for start in (0, PACK * H - H // 2)
+        ]
+        w_codes = [keep.tile([P, H], U32, name="w_codes_%d" % c, align_bytes=64) for c in range(PASSES)]
+        w_plane = [keep.tile([P, H], U8, name="w_plane_%d" % c, align_bytes=64) for c in range(PASSES)]
+
+        def cast_x(copy, c, u, lo, raw, a, b):
+            dst = pairs[c, u][:].bitcast(BF16).rearrange("p (n e) -> p n e", e=2)
+            copy(dst[:, lo + a : lo + b, :], raw[:, :, a:b].rearrange("p e n -> p n e"))
+
+        shares = {0: 512, 1: 320, 7: 160}
+        for i, (c, u, lo, hi, raw) in enumerate(x_pieces):
+            width = hi - lo
+            share = shares.get(i, 0)
+            if share:
+                cast_x(vector_copy, c, u, lo, raw, 0, share)
+            if share < width:
+                cast_x(scalar_copy, c, u, lo, raw, share, width)
+            if hi == T and u == 0:
+                nc.vector.tensor_copy(out=picked[c][:, 0, :], in_=pairs[c, 0][:].indirect(offsets[:]))
+            if hi == T and u == 1:
+                halves = [slice(a * HALF, (a + 1) * HALF) for a in range(2)]
+                for a, tokens in enumerate(halves):
+                    entries = offsets[:, a * HALF // 16 : (a + 1) * HALF // 16]
+                    nc.vector.tensor_copy(out=picked[c][:, 1, tokens], in_=pairs[c, 1][:].indirect(entries))
+                for tokens in halves:
+                    nc.vector.tensor_copy(
+                        out=x_bf[c][:].bitcast(I32).rearrange("p (n u) -> p n u", u=2)[:, tokens, :],
+                        in_=picked[c][:, :, tokens].bitcast(I32).rearrange("p u n -> p n u"),
+                    )
+                for a, tokens in enumerate(halves):
+                    nc.vector.quantize_mx(
+                        out=x_codes[c][:, tokens].bitcast(FP8X4),
+                        scales=x_plane[c][:, tokens],
+                        in_=x_bf[c][:, a * HALF * PACK : (a + 1) * HALF * PACK],
+                    )
+
+        def cast_w(copy, c, g, t0=0, t1=PACK):
+            copy(
+                w_bf[c][:, t0:t1, g * 64 : (g + 1) * 64, :].rearrange("p t m j -> p m j t"),
+                w_raw[c, g][:].rearrange("p j (m t) -> p m j t", t=PACK)[:, :, :, t0:t1],
+            )
+
+        def quantize_w(c, t):
+            cols = slice(t * P, (t + 1) * P)
+            nc.vector.quantize_mx(
+                out=w_codes[c][:, cols].bitcast(FP8X4),
+                scales=w_plane[c][:, cols],
+                in_=w_bf[c][:, t, :, :].rearrange("p m j -> p (m j)"),
+            )
+
+        h = {(a, t): psum.tile([P, HALF], F32, name="bank_%d_%d" % (a, t)) for a in range(2) for t in range(PACK)}
+
+        def first_product(c, a, t):
+            cols = slice(t * P, (t + 1) * P)
+            tokens = slice(a * HALF, (a + 1) * HALF)
+            nc.tensor.matmul_mx(
+                out=h[a, t][:],
+                lhsT=w_codes[c][:, cols].bitcast(FP8X4),
+                lhsT_scale=w_plane[c][:, cols],
+                rhs=x_codes[c][:, tokens].bitcast(FP8X4),
+                rhs_scale=x_plane[c][:, tokens],
+                start=(c == 0),
+                stop=(c == PASSES - 1),
+            )
+
+        cast_w(scalar_copy, 0, 1)
+        cast_w(scalar_copy, 0, 0)
+        for t in range(PACK):
+            quantize_w(0, t)
+        cast_w(scalar_copy, 1, 1)
+        cast_w(vector_copy, 1, 0, 0, 2)
+        cast_w(scalar_copy, 1, 0, 2, 4)
+        for t in range(PACK):
+            quantize_w(1, t)
+        for a in range(2):
+            for c in range(PASSES):
+                for t in range(PACK):
+                    first_product(c, a, t)
+
+        z_rows = [keep.tile([P, PACK, HALF], BF16, name="z_rows_%d" % a) for a in range(2)]
+        z_bf = [keep.tile([P, HALF * PACK], BF16, name="z_bf_%d" % a, align_bytes=64) for a in range(2)]
+        z_codes = [keep.tile([P, HALF], U32, name="z_codes_%d" % a, align_bytes=64) for a in range(2)]
+        z_plane = [keep.tile([P, HALF], U8, name="z_plane_%d" % a, align_bytes=64) for a in range(2)]
+        for a in range(2):
+            j0 = a * HALF
+            for t in range(PACK):
+                nc.scalar.activation(
+                    out=delayed[:, t, j0 + 1 : j0 + 1 + HALF], in_=h[a, t][:], func=COPY, scale=tap[:, t, 1:2]
+                )
+                nc.vector.scalar_tensor_tensor(
+                    out=z_rows[a][:, t, :],
+                    in0=h[a, t][:],
+                    scalar=tap[:, t, 0:1],
+                    in1=delayed[:, t, j0 : j0 + HALF],
+                    op0=MULT,
+                    op1=ADD,
+                )
+
+        def weave_z(copy, a):
+            copy(
+                z_bf[a][:].rearrange("p (c i t) -> p c t i", i=4, t=PACK),
+                z_rows[a][:].rearrange("p t (c i) -> p c t i", i=4),
+            )
+
+        weave_z(lambda dst, src: nc.scalar.copy(out=dst, in_=src), 0)
+        weave_z(vector_copy, 1)
+        for a, copy in ((1, scalar_copy), (0, vector_copy)):
+            nc.vector.quantize_mx(out=z_codes[a][:].bitcast(FP8X4), scales=z_plane[a][:], in_=z_bf[a][:])
+            acc = psum.tile([P, HALF], F32, name="bank_0_%d" % a)
+            nc.tensor.matmul_mx(
+                out=acc[:],
+                lhsT=w2_codes[:].bitcast(FP4X4),
+                lhsT_scale=w2_plane[:],
+                rhs=z_codes[a][:].bitcast(FP8X4),
+                rhs_scale=z_plane[a][:],
+                start=True,
+                stop=True,
+            )
+            result = keep.tile([P, HALF], F32, name="result_%d" % a)
+            copy(result[:], acc[:])
+            nc.sync.dma_start(out=out[:, a * HALF : (a + 1) * HALF], in_=result[:])

@@ -46,116 +46,133 @@ def tile_picked_dconv_none_e_kernel(tc, xT, w1, w2_words, w2_scales, taps, offs,
         nc.vector.memset(w2_plane[:].bitcast(I32), 0)
         nc.vector.memset(delayed[:, :, 0:1], 0.0)
 
-        x_pieces = []
+        x_raw = {}
         for c in range(PASSES):
             rows = xT[c * K_PASS : (c + 1) * K_PASS, :].rearrange("(p u e) n -> p u e n", u=2, e=2)
             for u in range(2):
-                for lo, hi in ((0, T // 2), (T // 2, T)):
-                    raw = keep.tile([P, 2, hi - lo], F32, name="x_raw_%d_%d_%d" % (c, u, lo))
-                    nc.sync.dma_start(out=raw[:], in_=rows[:, u, :, lo:hi])
-                    x_pieces.append((c, u, lo, hi, raw))
+                x_raw[c, u] = keep.tile([P, 2, T], F32, name="x_raw_%d_%d" % (c, u))
+                nc.sync.dma_start(out=x_raw[c, u][:], in_=rows[:, u, :, :])
                 if c == 0 and u == 0:
                     nc.sync.dma_start(offsets[:], offs)
-        w_raw = {}
+        w_raw = []
         for c in range(PASSES):
-            rows = w1[c * K_PASS : (c + 1) * K_PASS, :].rearrange("(p j) n -> p j n", j=PACK)
-            if c == PASSES - 1:
-                nc.sync.dma_start(out=tap[:], in_=taps.rearrange("(p t) d -> p t d", t=PACK))
-            for g in (1, 0):
-                w_raw[c, g] = keep.tile([P, PACK, H // 2], F32, name="w_raw_%d_%d" % (c, g))
-                nc.sync.dma_start(out=w_raw[c, g][:], in_=rows[:, :, g * (H // 2) : (g + 1) * (H // 2)])
+            w_raw.append(keep.tile([P, PACK, H], F32, name="w_raw_%d" % c, align_bytes=64))
+            nc.sync.dma_start(
+                out=w_raw[c][:], in_=w1[c * K_PASS : (c + 1) * K_PASS, :].rearrange("(p j) n -> p j n", j=PACK)
+            )
+        nc.sync.dma_start(out=tap[:], in_=taps.rearrange("(p t) d -> p t d", t=PACK))
         nc.sync.dma_start(out=w2_codes[:].bitcast(I32), in_=w2_words[0].bitcast(I32))
         for q in range(4):
             nc.sync.dma_start(
                 out=w2_plane[32 * q : 32 * q + 4, :].bitcast(I32), in_=w2_scales[0, 4 * q : 4 * q + 4, :].bitcast(I32)
             )
 
-        pairs = {(c, u): keep.tile([P, T], U32, name="pairs_%d_%d" % (c, u)) for c in range(PASSES) for u in range(2)}
-        picked = [keep.tile([P, 2, S], U32, name="picked_%d" % c) for c in range(PASSES)]
-        x_bf = [keep.tile([P, S * PACK], BF16, name="x_bf_%d" % c, align_bytes=64) for c in range(PASSES)]
+        OVER = 16
+        early = keep.tile([P, 2 * T - OVER], U32, name="early", align_bytes=64)
+        middle = keep.tile([P, T], U32, name="middle")
+        late = keep.tile([P, T + S + 2 * S - 2 * OVER], U32, name="late", align_bytes=64)
+        pairs = {(0, 0): early[:, 0:T], (0, 1): early[:, T - OVER :], (1, 0): middle[:], (1, 1): late[:, 0:T]}
+        picked_0 = keep.tile([P, 2 * S], U32, name="picked_0")
+        picked = [ap.rearrange("p (u n) -> p u n", u=2) for ap in (picked_0[:], late[:, T + S - 2 * OVER :])]
+        x_quads = {(0, 0): late[:, T - OVER : T - OVER + S]}
+        for c, a in ((0, 1), (1, 0), (1, 1)):
+            quads = keep.tile([P, S], U32, name="x_quads_%d_%d" % (c, a), align_bytes=64)
+            x_quads[c, a] = quads[:]
         x_codes = [keep.tile([P, S], U32, name="x_codes_%d" % c, align_bytes=64) for c in range(PASSES)]
         x_plane = [keep.tile([P, S], U8, name="x_plane_%d" % c, align_bytes=64) for c in range(PASSES)]
-        w_both = keep.tile([P, 2 * PACK * H - H // 2], BF16, name="w_both", align_bytes=64)
-        w_bf = [
-            w_both[:, start : start + PACK * H].rearrange("p (t m j) -> p t m j", t=PACK, j=PACK)
-            for start in (0, PACK * H - H // 2)
-        ]
-        w_codes = [keep.tile([P, H], U32, name="w_codes_%d" % c, align_bytes=64) for c in range(PASSES)]
-        w_plane = [keep.tile([P, H], U8, name="w_plane_%d" % c, align_bytes=64) for c in range(PASSES)]
+        halves = [slice(a * HALF, (a + 1) * HALF) for a in range(2)]
 
-        def cast_x(copy, c, u, lo, raw, a, b):
-            dst = pairs[c, u][:].bitcast(BF16).rearrange("p (n e) -> p n e", e=2)
-            copy(dst[:, lo + a : lo + b, :], raw[:, :, a:b].rearrange("p e n -> p n e"))
+        def cast_x(copy, c, u, lo, hi):
+            dst = pairs[c, u].bitcast(BF16).rearrange("p (n e) -> p n e", e=2)
+            copy(dst[:, lo:hi, :], x_raw[c, u][:, :, lo:hi].rearrange("p e n -> p n e"))
 
-        shares = {0: 512, 1: 320, 7: 160}
-        for i, (c, u, lo, hi, raw) in enumerate(x_pieces):
-            width = hi - lo
-            share = shares.get(i, 0)
-            if share:
-                cast_x(vector_copy, c, u, lo, raw, 0, share)
-            if share < width:
-                cast_x(scalar_copy, c, u, lo, raw, share, width)
-            if hi == T and u == 0:
-                nc.vector.tensor_copy(out=picked[c][:, 0, :], in_=pairs[c, 0][:].indirect(offsets[:]))
-            if hi == T and u == 1:
-                halves = [slice(a * HALF, (a + 1) * HALF) for a in range(2)]
-                for a, tokens in enumerate(halves):
-                    entries = offsets[:, a * HALF // 16 : (a + 1) * HALF // 16]
-                    nc.vector.tensor_copy(out=picked[c][:, 1, tokens], in_=pairs[c, 1][:].indirect(entries))
-                for tokens in halves:
-                    nc.vector.tensor_copy(
-                        out=x_bf[c][:].bitcast(I32).rearrange("p (n u) -> p n u", u=2)[:, tokens, :],
-                        in_=picked[c][:, :, tokens].bitcast(I32).rearrange("p u n -> p n u"),
-                    )
-                for a, tokens in enumerate(halves):
-                    nc.vector.quantize_mx(
-                        out=x_codes[c][:, tokens].bitcast(FP8X4),
-                        scales=x_plane[c][:, tokens],
-                        in_=x_bf[c][:, a * HALF * PACK : (a + 1) * HALF * PACK],
-                    )
+        def gather_whole(c):
+            nc.vector.tensor_copy(out=picked[c][:, 0, :], in_=pairs[c, 0].indirect(offsets[:]))
 
-        def cast_w(copy, c, g, t0=0, t1=PACK):
-            copy(
-                w_bf[c][:, t0:t1, g * 64 : (g + 1) * 64, :].rearrange("p t m j -> p m j t"),
-                w_raw[c, g][:].rearrange("p j (m t) -> p m j t", t=PACK)[:, :, :, t0:t1],
+        def finish_x(c):
+            for a, tokens in enumerate(halves):
+                entries = offsets[:, a * HALF // 16 : (a + 1) * HALF // 16]
+                nc.vector.tensor_copy(out=picked[c][:, 1, tokens], in_=pairs[c, 1].indirect(entries))
+            for a, tokens in enumerate(halves):
+                nc.vector.tensor_copy(
+                    out=x_quads[c, a].bitcast(I32).rearrange("p (n u) -> p n u", u=2),
+                    in_=picked[c][:, :, tokens].bitcast(I32).rearrange("p u n -> p n u"),
+                )
+
+        def quantize_x(c, a):
+            nc.vector.quantize_mx(
+                out=x_codes[c][:, halves[a]].bitcast(FP8X4),
+                scales=x_plane[c][:, halves[a]],
+                in_=x_quads[c, a].bitcast(BF16),
             )
 
-        def quantize_w(c, t):
-            cols = slice(t * P, (t + 1) * P)
+        cast_x(scalar_copy, 0, 0, 672, T)
+        cast_x(vector_copy, 0, 0, 0, 672)
+        gather_whole(0)
+        cast_x(scalar_copy, 0, 1, 672, T)
+        cast_x(vector_copy, 0, 1, 0, 672)
+        finish_x(0)
+        quantize_x(0, 0)
+        quantize_x(0, 1)
+        cast_x(scalar_copy, 1, 0, 0, T)
+        cast_x(scalar_copy, 1, 1, 0, T - 296)
+        cast_x(vector_copy, 1, 1, T - 296, T)
+        gather_whole(1)
+        finish_x(1)
+        quantize_x(1, 0)
+
+        w_codes = [keep.tile([P, H], U32, name="w_codes_%d" % c, align_bytes=64) for c in range(PASSES)]
+        w_bf, w_plane = {}, {}
+
+        def cast_w(copy, c, g, tag):
+            w_bf[c, g] = keep.tile([P, 2, P, PACK], BF16, name="w_bf_%d_%d" % (c, g), tag=tag, align_bytes=64)
+            copy(
+                w_bf[c, g][:].rearrange("p t m j -> p m j t"),
+                w_raw[c][:].rearrange("p j (m t) -> p m j t", t=PACK)[:, :, :, 2 * g : 2 * g + 2],
+            )
+
+        def quantize_w(c, t0, t1):
+            cols = slice(t0 * P, t1 * P)
             nc.vector.quantize_mx(
                 out=w_codes[c][:, cols].bitcast(FP8X4),
-                scales=w_plane[c][:, cols],
-                in_=w_bf[c][:, t, :, :].rearrange("p m j -> p (m j)"),
+                scales=w_plane[c, t0 // 2][:, (t0 % 2) * P : (t0 % 2 + t1 - t0) * P],
+                in_=w_bf[c, t0 // 2][:, t0 % 2 : t0 % 2 + t1 - t0, :, :].rearrange("p t m j -> p (t m j)"),
             )
 
         h = {(a, t): psum.tile([P, HALF], F32, name="bank_%d_%d" % (a, t)) for a in range(2) for t in range(PACK)}
 
-        def first_product(c, a, t):
+        def first_product(c, a, t, first):
             cols = slice(t * P, (t + 1) * P)
             tokens = slice(a * HALF, (a + 1) * HALF)
             nc.tensor.matmul_mx(
                 out=h[a, t][:],
                 lhsT=w_codes[c][:, cols].bitcast(FP8X4),
-                lhsT_scale=w_plane[c][:, cols],
+                lhsT_scale=w_plane[c, t // 2][:, (t % 2) * P : (t % 2 + 1) * P],
                 rhs=x_codes[c][:, tokens].bitcast(FP8X4),
                 rhs_scale=x_plane[c][:, tokens],
-                start=(c == 0),
-                stop=(c == PASSES - 1),
+                start=first,
+                stop=not first,
             )
 
-        cast_w(scalar_copy, 0, 1)
-        cast_w(scalar_copy, 0, 0)
-        for t in range(PACK):
-            quantize_w(0, t)
-        cast_w(scalar_copy, 1, 1)
-        cast_w(vector_copy, 1, 0, 0, 2)
-        cast_w(scalar_copy, 1, 0, 2, 4)
-        for t in range(PACK):
-            quantize_w(1, t)
+        cast_w(scalar_copy, 0, 0, "w_bf_first")
+        plane_0 = keep.tile([P, H], U8, name="w_plane_0", tag="late", align_bytes=64)
+        w_plane[0, 0], w_plane[0, 1] = plane_0[:, 0 : H // 2], plane_0[:, H // 2 : H]
+        quantize_w(0, 0, 2)
+        quantize_x(1, 1)
+        cast_w(scalar_copy, 0, 1, "w_bf_0_1")
+        quantize_w(0, 2, 4)
+        cast_w(vector_copy, 1, 0, "w_bf_first")
+        cast_w(scalar_copy, 1, 1, "w_bf_1_1")
+        w_plane[1, 0] = keep.tile([P, H // 2], U8, name="w_plane_1_0", align_bytes=64)
+        quantize_w(1, 0, 1)
+        quantize_w(1, 1, 2)
+        w_plane[1, 1] = keep.tile([P, H // 2], U8, name="w_plane_1_1", tag="w_raw_1", align_bytes=64)
+        quantize_w(1, 2, 4)
         for a in range(2):
-            for c in range(PASSES):
-                for t in range(PACK):
-                    first_product(c, a, t)
+            for t in range(PACK):
+                order = (1, 0) if a == 1 and t >= 1 else (0, 1)
+                first_product(order[0], a, t, True)
+                first_product(order[1], a, t, False)
 
         z_rows = [keep.tile([P, PACK, HALF], BF16, name="z_rows_%d" % a) for a in range(2)]
         z_bf = [keep.tile([P, HALF * PACK], BF16, name="z_bf_%d" % a, align_bytes=64) for a in range(2)]

@@ -50,7 +50,7 @@ def tile_picked_dconv_none_e_kernel(tc, xT, w1, w2_words, w2_scales, taps, offs,
         for c in range(PASSES):
             rows = xT[c * K_PASS : (c + 1) * K_PASS, :].rearrange("(p u e) n -> p u e n", u=2, e=2)
             for u in range(2):
-                x_raw[c, u] = keep.tile([P, 2, T], F32, name="x_raw_%d_%d" % (c, u))
+                x_raw[c, u] = keep.tile([P, 2, T], F32, name="x_raw_%d_%d" % (c, u), align_bytes=64)
                 nc.sync.dma_start(out=x_raw[c, u][:], in_=rows[:, u, :, :])
                 if c == 0 and u == 0:
                     nc.sync.dma_start(offsets[:], offs)
@@ -68,18 +68,16 @@ def tile_picked_dconv_none_e_kernel(tc, xT, w1, w2_words, w2_scales, taps, offs,
             )
 
         OVER = 16
-        early = keep.tile([P, 2 * T - OVER], U32, name="early", align_bytes=64)
-        middle = keep.tile([P, T], U32, name="middle")
-        late = keep.tile([P, T + S + 2 * S - 2 * OVER], U32, name="late", align_bytes=64)
-        pairs = {(0, 0): early[:, 0:T], (0, 1): early[:, T - OVER :], (1, 0): middle[:], (1, 1): late[:, 0:T]}
-        picked_0 = keep.tile([P, 2 * S], U32, name="picked_0")
-        picked = [ap.rearrange("p (u n) -> p u n", u=2) for ap in (picked_0[:], late[:, T + S - 2 * OVER :])]
-        x_quads = {(0, 0): late[:, T - OVER : T - OVER + S]}
-        for c, a in ((0, 1), (1, 0), (1, 1)):
-            quads = keep.tile([P, S], U32, name="x_quads_%d_%d" % (c, a), align_bytes=64)
-            x_quads[c, a] = quads[:]
+        early = keep.tile([P, 2 * T - OVER], U32, name="early")
+        pairs = {(0, 0): early[:, 0:T], (0, 1): early[:, T - OVER :]}
+        for u in range(2):
+            window = keep.tile([P, T], U32, name="pairs_1_%d" % u, align_bytes=64)
+            pairs[1, u] = window[:]
+        picked = [keep.tile([P, 2, S], U32, name="picked_%d" % c) for c in range(PASSES)]
+        x_quads, x_plane = {}, {}
+        quads = keep.tile([P, S], U32, name="x_quads_1_0", align_bytes=64)
+        x_quads[1, 0] = quads[:]
         x_codes = [keep.tile([P, S], U32, name="x_codes_%d" % c, align_bytes=64) for c in range(PASSES)]
-        x_plane = [keep.tile([P, S], U8, name="x_plane_%d" % c, align_bytes=64) for c in range(PASSES)]
         halves = [slice(a * HALF, (a + 1) * HALF) for a in range(2)]
 
         def cast_x(copy, c, u, lo, hi):
@@ -93,33 +91,45 @@ def tile_picked_dconv_none_e_kernel(tc, xT, w1, w2_words, w2_scales, taps, offs,
             for a, tokens in enumerate(halves):
                 entries = offsets[:, a * HALF // 16 : (a + 1) * HALF // 16]
                 nc.vector.tensor_copy(out=picked[c][:, 1, tokens], in_=pairs[c, 1].indirect(entries))
-            for a, tokens in enumerate(halves):
-                nc.vector.tensor_copy(
-                    out=x_quads[c, a].bitcast(I32).rearrange("p (n u) -> p n u", u=2),
-                    in_=picked[c][:, :, tokens].bitcast(I32).rearrange("p u n -> p n u"),
-                )
 
-        def quantize_x(c, a):
+        def weave_x(c, a):
+            nc.vector.tensor_copy(
+                out=x_quads[c, a].bitcast(I32).rearrange("p (n u) -> p n u", u=2),
+                in_=picked[c][:, :, halves[a]].bitcast(I32).rearrange("p u n -> p n u"),
+            )
+
+        def quantize_x(c, a, tag):
+            x_plane[c, a] = keep.tile([P, HALF], U8, name="x_plane_%d_%d" % (c, a), tag=tag, align_bytes=64)
             nc.vector.quantize_mx(
                 out=x_codes[c][:, halves[a]].bitcast(FP8X4),
-                scales=x_plane[c][:, halves[a]],
+                scales=x_plane[c, a][:],
                 in_=x_quads[c, a].bitcast(BF16),
             )
 
-        cast_x(scalar_copy, 0, 0, 672, T)
-        cast_x(vector_copy, 0, 0, 0, 672)
+        def cast_shared(c, u, share):
+            cast_x(scalar_copy, c, u, share, T)
+            cast_x(vector_copy, c, u, 0, share)
+
+        cast_shared(0, 0, 672)
         gather_whole(0)
-        cast_x(scalar_copy, 0, 1, 672, T)
-        cast_x(vector_copy, 0, 1, 0, 672)
+        cast_shared(0, 1, 672)
         finish_x(0)
-        quantize_x(0, 0)
-        quantize_x(0, 1)
-        cast_x(scalar_copy, 1, 0, 0, T)
-        cast_x(scalar_copy, 1, 1, 0, T - 296)
-        cast_x(vector_copy, 1, 1, T - 296, T)
+        cast_shared(1, 0, 600)
         gather_whole(1)
+        quads_0 = keep.tile([P, S, 2], U32, name="x_quads_0", tag="x_raw_1_0", align_bytes=64)
+        nc.scalar.copy(out=quads_0[:], in_=picked[0][:].rearrange("p u n -> p n u"))
+        cast_shared(1, 1, 528)
         finish_x(1)
-        quantize_x(1, 0)
+        weave_x(1, 0)
+        plane_0 = keep.tile([P, S], U8, name="x_plane_0", tag="pairs_1_1", align_bytes=64)
+        nc.vector.quantize_mx(
+            out=x_codes[0][:].bitcast(FP8X4),
+            scales=plane_0[:],
+            in_=quads_0[:].rearrange("p n u -> p (n u)").bitcast(BF16),
+        )
+        for a in range(2):
+            x_plane[0, a] = plane_0[:, halves[a]]
+        quantize_x(1, 0, "x_plane_1_0")
 
         w_codes = [keep.tile([P, H], U32, name="w_codes_%d" % c, align_bytes=64) for c in range(PASSES)]
         w_bf, w_plane = {}, {}
@@ -149,28 +159,43 @@ def tile_picked_dconv_none_e_kernel(tc, xT, w1, w2_words, w2_scales, taps, offs,
                 lhsT=w_codes[c][:, cols].bitcast(FP8X4),
                 lhsT_scale=w_plane[c, t // 2][:, (t % 2) * P : (t % 2 + 1) * P],
                 rhs=x_codes[c][:, tokens].bitcast(FP8X4),
-                rhs_scale=x_plane[c][:, tokens],
+                rhs_scale=x_plane[c, a][:],
                 start=first,
                 stop=not first,
             )
 
-        cast_w(scalar_copy, 0, 0, "w_bf_first")
-        plane_0 = keep.tile([P, H], U8, name="w_plane_0", tag="late", align_bytes=64)
-        w_plane[0, 0], w_plane[0, 1] = plane_0[:, 0 : H // 2], plane_0[:, H // 2 : H]
+        for c in range(PASSES):
+            plane = keep.tile([P, H], U8, name="w_plane_%d" % c, align_bytes=64)
+            w_plane[c, 0], w_plane[c, 1] = plane[:, 0 : H // 2], plane[:, H // 2 : H]
+        cast_w(scalar_copy, 0, 0, "w_bf_0_0")
         quantize_w(0, 0, 2)
-        quantize_x(1, 1)
         cast_w(scalar_copy, 0, 1, "w_bf_0_1")
-        quantize_w(0, 2, 4)
-        cast_w(vector_copy, 1, 0, "w_bf_first")
+        cast_w(vector_copy, 1, 0, "w_bf_1_0")
         cast_w(scalar_copy, 1, 1, "w_bf_1_1")
-        w_plane[1, 0] = keep.tile([P, H // 2], U8, name="w_plane_1_0", align_bytes=64)
+        quantize_w(0, 2, 4)
         quantize_w(1, 0, 1)
         quantize_w(1, 1, 2)
-        w_plane[1, 1] = keep.tile([P, H // 2], U8, name="w_plane_1_1", tag="w_raw_1", align_bytes=64)
+        last_quads = keep.tile([P, S], U32, name="x_quads_1_1", tag="w_raw_1", align_bytes=64)
+        x_quads[1, 1] = last_quads[:]
+        nc.scalar.copy(
+            out=last_quads[:].rearrange("p (n u) -> p n u", u=2),
+            in_=picked[1][:, :, halves[1]].rearrange("p u n -> p n u"),
+        )
         quantize_w(1, 2, 4)
+        quantize_x(1, 1, "x_plane_1_1")
+        for warm in range(3):
+            nc.tensor.matmul_mx(
+                out=h[1, 3][:],
+                lhsT=x_codes[0][:, HALF : HALF + P].bitcast(FP8X4),
+                lhsT_scale=x_plane[0, 1][:, 0:P],
+                rhs=x_codes[0][:, HALF:].bitcast(FP8X4),
+                rhs_scale=x_plane[0, 1][:],
+                start=True,
+                stop=True,
+            )
         for a in range(2):
             for t in range(PACK):
-                order = (1, 0) if a == 1 and t >= 1 else (0, 1)
+                order = (1, 0) if t >= 2 else (0, 1)
                 first_product(order[0], a, t, True)
                 first_product(order[1], a, t, False)
 
@@ -201,7 +226,7 @@ def tile_picked_dconv_none_e_kernel(tc, xT, w1, w2_words, w2_scales, taps, offs,
 
         weave_z(lambda dst, src: nc.scalar.copy(out=dst, in_=src), 0)
         weave_z(vector_copy, 1)
-        for a, copy in ((1, scalar_copy), (0, vector_copy)):
+        for a, copy in ((0, scalar_copy), (1, vector_copy)):
             nc.vector.quantize_mx(out=z_codes[a][:].bitcast(FP8X4), scales=z_plane[a][:], in_=z_bf[a][:])
             acc = psum.tile([P, HALF], F32, name="bank_0_%d" % a)
             nc.tensor.matmul_mx(

@@ -118,17 +118,13 @@ def tile_picked_dconv_none_e_kernel(tc, xT, w1, w2_words, w2_scales, taps, offs,
         gather_whole(1)
         quads_0 = keep.tile([P, S, 2], U32, name="x_quads_0", tag="x_raw_1_0", align_bytes=64)
         nc.scalar.copy(out=quads_0[:], in_=picked[0][:].rearrange("p u n -> p n u"))
-        cast_shared(1, 1, 528)
+        for a in range(2):
+            x_quads[0, a] = quads_0[:, halves[a], :].rearrange("p n u -> p (n u)")
+        cast_shared(1, 1, 640)
+        quantize_x(0, 0, "x_raw_1_1")
         finish_x(1)
         weave_x(1, 0)
-        plane_0 = keep.tile([P, S], U8, name="x_plane_0", tag="pairs_1_1", align_bytes=64)
-        nc.vector.quantize_mx(
-            out=x_codes[0][:].bitcast(FP8X4),
-            scales=plane_0[:],
-            in_=quads_0[:].rearrange("p n u -> p (n u)").bitcast(BF16),
-        )
-        for a in range(2):
-            x_plane[0, a] = plane_0[:, halves[a]]
+        quantize_x(0, 1, "pairs_1_1")
         quantize_x(1, 0, "x_plane_1_0")
 
         w_codes = [keep.tile([P, H], U32, name="w_codes_%d" % c, align_bytes=64) for c in range(PASSES)]
@@ -199,7 +195,7 @@ def tile_picked_dconv_none_e_kernel(tc, xT, w1, w2_words, w2_scales, taps, offs,
                 first_product(order[0], a, t, True)
                 first_product(order[1], a, t, False)
 
-        z_rows = [keep.tile([P, PACK, HALF], BF16, name="z_rows_%d" % a) for a in range(2)]
+        z_rows = [keep.tile([P, PACK, HALF], F32, name="z_rows_%d" % a) for a in range(2)]
         z_bf = [keep.tile([P, HALF * PACK], BF16, name="z_bf_%d" % a, align_bytes=64) for a in range(2)]
         z_codes = [keep.tile([P, HALF], U32, name="z_codes_%d" % a, align_bytes=64) for a in range(2)]
         z_plane = [keep.tile([P, HALF], U8, name="z_plane_%d" % a, align_bytes=64) for a in range(2)]

@@ -22,6 +22,7 @@ PACK = 4
 K_PASS = P * PACK
 PASSES = K // K_PASS
 HALF = S // 2
+QUARTER = S // 4
 
 
 def tile_picked_dconv_none_e_kernel(tc, xT, w1, w2_words, w2_scales, taps, offs, out):
@@ -35,6 +36,7 @@ def tile_picked_dconv_none_e_kernel(tc, xT, w1, w2_words, w2_scales, taps, offs,
 
     with ExitStack() as ctx:
         keep = ctx.enter_context(tc.tile_pool(name="keep", bufs=1))
+        stage = ctx.enter_context(tc.tile_pool(name="stage", bufs=1))
         psum = ctx.enter_context(tc.psum_pool(name="psum", bufs=1))
 
         offsets = keep.tile([P, S // 16], U16, name="offsets")
@@ -56,7 +58,7 @@ def tile_picked_dconv_none_e_kernel(tc, xT, w1, w2_words, w2_scales, taps, offs,
                     nc.sync.dma_start(offsets[:], offs)
         w_raw = []
         for c in range(PASSES):
-            w_raw.append(keep.tile([P, PACK, H], F32, name="w_raw_%d" % c, align_bytes=64))
+            w_raw.append(stage.tile([P, PACK, H], F32, name="w_raw_%d" % c, align_bytes=64, offset=8192 * c))
             nc.sync.dma_start(
                 out=w_raw[c][:], in_=w1[c * K_PASS : (c + 1) * K_PASS, :].rearrange("(p j) n -> p j n", j=PACK)
             )
@@ -125,16 +127,14 @@ def tile_picked_dconv_none_e_kernel(tc, xT, w1, w2_words, w2_scales, taps, offs,
         finish_x(1)
         weave_x(1, 0)
         quantize_x(0, 1, "pairs_1_1")
-        quantize_x(1, 0, "x_plane_1_0")
 
         w_codes = [keep.tile([P, H], U32, name="w_codes_%d" % c, align_bytes=64) for c in range(PASSES)]
         w_bf, w_plane = {}, {}
 
-        def cast_w(copy, c, g, tag):
-            w_bf[c, g] = keep.tile([P, 2, P, PACK], BF16, name="w_bf_%d_%d" % (c, g), tag=tag, align_bytes=64)
+        def cast_w(copy, c, g, m0, m1):
             copy(
-                w_bf[c, g][:].rearrange("p t m j -> p m j t"),
-                w_raw[c][:].rearrange("p j (m t) -> p m j t", t=PACK)[:, :, :, 2 * g : 2 * g + 2],
+                w_bf[c, g][:].rearrange("p t m j -> p m j t")[:, m0:m1, :, :],
+                w_raw[c][:].rearrange("p j (m t) -> p m j t", t=PACK)[:, m0:m1, :, 2 * g : 2 * g + 2],
             )
 
         def quantize_w(c, t0, t1):
@@ -145,95 +145,114 @@ def tile_picked_dconv_none_e_kernel(tc, xT, w1, w2_words, w2_scales, taps, offs,
                 in_=w_bf[c, t0 // 2][:, t0 % 2 : t0 % 2 + t1 - t0, :, :].rearrange("p t m j -> p (t m j)"),
             )
 
-        h = {(a, t): psum.tile([P, HALF], F32, name="bank_%d_%d" % (a, t)) for a in range(2) for t in range(PACK)}
+        groups = [(t, a * HALF, (a + 1) * HALF, "bank_%d_%d" % (a, t)) for a in range(2) for t in range(PACK)][:-1]
+        groups = groups + [(3, HALF, 3 * QUARTER, "bank_1_3"), (3, 3 * QUARTER, S, "bank_0_0")]
 
-        def first_product(c, a, t, first):
+        def first_product(acc, c, t, lo, hi, first):
             cols = slice(t * P, (t + 1) * P)
-            tokens = slice(a * HALF, (a + 1) * HALF)
             nc.tensor.matmul_mx(
-                out=h[a, t][:],
+                out=acc[:],
                 lhsT=w_codes[c][:, cols].bitcast(FP8X4),
                 lhsT_scale=w_plane[c, t // 2][:, (t % 2) * P : (t % 2 + 1) * P],
-                rhs=x_codes[c][:, tokens].bitcast(FP8X4),
-                rhs_scale=x_plane[c, a][:],
+                rhs=x_codes[c][:, lo:hi].bitcast(FP8X4),
+                rhs_scale=x_plane[c, lo // HALF][:, lo % HALF : lo % HALF + hi - lo],
                 start=first,
                 stop=not first,
             )
 
+        for c, g in ((0, 0), (1, 0), (1, 1)):
+            plane = keep.tile([P, H // 2], U8, name="w_plane_%d_%d" % (c, g), align_bytes=64)
+            w_plane[c, g] = plane[:]
+        plane = stage.tile([P, H // 2], U8, name="w_plane_0_1", align_bytes=64, offset=12288)
+        w_plane[0, 1] = plane[:]
         for c in range(PASSES):
-            plane = keep.tile([P, H], U8, name="w_plane_%d" % c, align_bytes=64)
-            w_plane[c, 0], w_plane[c, 1] = plane[:, 0 : H // 2], plane[:, H // 2 : H]
-        cast_w(scalar_copy, 0, 0, "w_bf_0_0")
+            for g in range(2):
+                w_bf[c, g] = keep.tile([P, 2, P, PACK], BF16, name="w_bf_%d_%d" % (c, g), align_bytes=64)
+        cast_w(scalar_copy, 0, 0, 0, P)
         quantize_w(0, 0, 2)
-        cast_w(scalar_copy, 0, 1, "w_bf_0_1")
-        cast_w(vector_copy, 1, 0, "w_bf_1_0")
-        cast_w(scalar_copy, 1, 1, "w_bf_1_1")
-        quantize_w(0, 2, 4)
+        quantize_x(1, 0, "w_bf_0_0")
+        cast_w(scalar_copy, 0, 1, 0, P)
+        cast_w(scalar_copy, 1, 0, 86, P)
+        cast_w(vector_copy, 1, 0, 0, 86)
+        cast_w(scalar_copy, 1, 1, 78, P)
+        cast_w(vector_copy, 1, 1, 0, 78)
         quantize_w(1, 0, 1)
         quantize_w(1, 1, 2)
-        last_quads = keep.tile([P, S], U32, name="x_quads_1_1", tag="w_raw_1", align_bytes=64)
+        quantize_w(0, 2, 4)
+        quantize_w(1, 2, 3)
+        quantize_w(1, 3, 4)
+        last_quads = stage.tile([P, S], U32, name="x_quads_1_1", align_bytes=64, offset=8192)
         x_quads[1, 1] = last_quads[:]
         nc.scalar.copy(
             out=last_quads[:].rearrange("p (n u) -> p n u", u=2),
             in_=picked[1][:, :, halves[1]].rearrange("p u n -> p n u"),
         )
-        quantize_w(1, 2, 4)
         quantize_x(1, 1, "x_plane_1_1")
-        for warm in range(3):
-            nc.tensor.matmul_mx(
-                out=h[1, 3][:],
-                lhsT=x_codes[0][:, HALF : HALF + P].bitcast(FP8X4),
-                lhsT_scale=x_plane[0, 1][:, 0:P],
-                rhs=x_codes[0][:, HALF:].bitcast(FP8X4),
-                rhs_scale=x_plane[0, 1][:],
-                start=True,
-                stop=True,
-            )
-        for a in range(2):
-            for t in range(PACK):
-                order = (1, 0) if t >= 2 else (0, 1)
-                first_product(order[0], a, t, True)
-                first_product(order[1], a, t, False)
 
         z_rows = [keep.tile([P, PACK, HALF], F32, name="z_rows_%d" % a) for a in range(2)]
-        z_bf = [keep.tile([P, HALF * PACK], BF16, name="z_bf_%d" % a, align_bytes=64) for a in range(2)]
-        z_codes = [keep.tile([P, HALF], U32, name="z_codes_%d" % a, align_bytes=64) for a in range(2)]
-        z_plane = [keep.tile([P, HALF], U8, name="z_plane_%d" % a, align_bytes=64) for a in range(2)]
-        for a in range(2):
-            j0 = a * HALF
-            for t in range(PACK):
-                nc.scalar.activation(
-                    out=delayed[:, t, j0 + 1 : j0 + 1 + HALF], in_=h[a, t][:], func=COPY, scale=tap[:, t, 1:2]
-                )
-                nc.vector.scalar_tensor_tensor(
-                    out=z_rows[a][:, t, :],
-                    in0=h[a, t][:],
-                    scalar=tap[:, t, 0:1],
-                    in1=delayed[:, t, j0 : j0 + HALF],
-                    op0=MULT,
-                    op1=ADD,
-                )
-
-        def weave_z(copy, a):
-            copy(
-                z_bf[a][:].rearrange("p (c i t) -> p c t i", i=4, t=PACK),
-                z_rows[a][:].rearrange("p t (c i) -> p c t i", i=4),
+        z_bf = keep.tile([P, S * PACK], BF16, name="z_bf", align_bytes=64)
+        z_codes = keep.tile([P, S], U32, name="z_codes", align_bytes=64)
+        z_plane = keep.tile([P, S], U8, name="z_plane", align_bytes=64)
+        for t, lo, hi, bank in groups:
+            h = psum.tile([P, hi - lo], F32, name="h_%d_%d" % (t, lo), tag=bank)
+            order = (1, 0) if t >= 2 else (0, 1)
+            first_product(h, order[0], t, lo, hi, True)
+            first_product(h, order[1], t, lo, hi, False)
+            nc.scalar.activation(out=delayed[:, t, lo + 1 : hi + 1], in_=h[:], func=COPY, scale=tap[:, t, 1:2])
+            nc.vector.scalar_tensor_tensor(
+                out=z_rows[lo // HALF][:, t, lo % HALF : lo % HALF + hi - lo],
+                in0=h[:],
+                scalar=tap[:, t, 0:1],
+                in1=delayed[:, t, lo:hi],
+                op0=MULT,
+                op1=ADD,
             )
 
-        weave_z(lambda dst, src: nc.scalar.copy(out=dst, in_=src), 0)
-        weave_z(vector_copy, 1)
-        for a, copy in ((0, scalar_copy), (1, vector_copy)):
-            nc.vector.quantize_mx(out=z_codes[a][:].bitcast(FP8X4), scales=z_plane[a][:], in_=z_bf[a][:])
-            acc = psum.tile([P, HALF], F32, name="bank_0_%d" % a)
+        def weave_z(copy, q):
+            a, lo = q // 2, (q % 2) * QUARTER
+            copy(
+                z_bf[:, q * QUARTER * PACK : (q + 1) * QUARTER * PACK].rearrange("p (c i t) -> p c t i", i=4, t=PACK),
+                z_rows[a][:, :, lo : lo + QUARTER].rearrange("p t (c i) -> p c t i", i=4),
+            )
+
+        result = [keep.tile([P, HALF], F32, name="result_%d" % a) for a in range(2)]
+
+        def quantize_z(q):
+            lo, hi = q * QUARTER, (q + 1) * QUARTER
+            nc.vector.quantize_mx(
+                out=z_codes[:, lo:hi].bitcast(FP8X4), scales=z_plane[:, lo:hi], in_=z_bf[:, lo * PACK : hi * PACK]
+            )
+
+        def second_product(copy, lo, hi, bank):
+            acc = psum.tile([P, hi - lo], F32, name="acc_%d" % lo, tag=bank)
             nc.tensor.matmul_mx(
                 out=acc[:],
                 lhsT=w2_codes[:].bitcast(FP4X4),
                 lhsT_scale=w2_plane[:],
-                rhs=z_codes[a][:].bitcast(FP8X4),
-                rhs_scale=z_plane[a][:],
+                rhs=z_codes[:, lo:hi].bitcast(FP8X4),
+                rhs_scale=z_plane[:, lo:hi],
                 start=True,
                 stop=True,
             )
-            result = keep.tile([P, HALF], F32, name="result_%d" % a)
-            copy(result[:], acc[:])
-            nc.sync.dma_start(out=out[:, a * HALF : (a + 1) * HALF], in_=result[:])
+            copy(result[lo // HALF][:, lo % HALF : lo % HALF + hi - lo], acc[:])
+
+        nc.gpsimd.tensor_scalar(
+            z_bf[:, 0 : QUARTER * PACK].rearrange("p (n t) -> p n t", t=PACK),
+            z_rows[0][:, :, 0:QUARTER].rearrange("p t n -> p n t"),
+            1.0,
+            0.0,
+            MULT,
+            ADD,
+        )
+        weave_z(scalar_copy, 1)
+        quantize_z(0)
+        weave_z(vector_copy, 3)
+        weave_z(scalar_copy, 2)
+        quantize_z(1)
+        second_product(scalar_copy, 0, HALF, "bank_0_3")
+        nc.sync.dma_start(out=out[:, 0:HALF], in_=result[0][:])
+        quantize_z(3)
+        quantize_z(2)
+        second_product(vector_copy, 3 * QUARTER, S, "bank_0_1")
+        second_product(vector_copy, HALF, 3 * QUARTER, "bank_0_2")
+        nc.sync.dma_start(out=out[:, HALF:S], in_=result[1][:])

@@ -120,13 +120,17 @@ def tile_picked_dconv_none_e_kernel(tc, xT, w1, w2_words, w2_scales, taps, offs,
         gather_whole(1)
         quads_0 = keep.tile([P, S, 2], U32, name="x_quads_0", tag="x_raw_1_0", align_bytes=64)
         nc.scalar.copy(out=quads_0[:], in_=picked[0][:].rearrange("p u n -> p n u"))
-        for a in range(2):
-            x_quads[0, a] = quads_0[:, halves[a], :].rearrange("p n u -> p (n u)")
         cast_shared(1, 1, 640)
-        quantize_x(0, 0, "x_raw_1_1")
+        plane_0 = keep.tile([P, S], U8, name="x_plane_0", tag="x_raw_1_1", align_bytes=64)
+        nc.vector.quantize_mx(
+            out=x_codes[0][:].bitcast(FP8X4),
+            scales=plane_0[:],
+            in_=quads_0[:].rearrange("p n u -> p (n u)").bitcast(BF16),
+        )
+        for a in range(2):
+            x_plane[0, a] = plane_0[:, halves[a]]
         finish_x(1)
         weave_x(1, 0)
-        quantize_x(0, 1, "pairs_1_1")
 
         w_codes = [keep.tile([P, H], U32, name="w_codes_%d" % c, align_bytes=64) for c in range(PASSES)]
         w_bf, w_plane = {}, {}
@@ -145,6 +149,17 @@ def tile_picked_dconv_none_e_kernel(tc, xT, w1, w2_words, w2_scales, taps, offs,
                 in_=w_bf[c, t0 // 2][:, t0 % 2 : t0 % 2 + t1 - t0, :, :].rearrange("p t m j -> p (t m j)"),
             )
 
+        warm = psum.tile([P, S], F32, name="warm", tag="bank_1_3")
+        for turn in range(2):
+            nc.tensor.matmul_mx(
+                out=warm[:],
+                lhsT=x_codes[0][:, 0:P].bitcast(FP8X4),
+                lhsT_scale=plane_0[:, 0:P],
+                rhs=x_codes[0][:].bitcast(FP8X4),
+                rhs_scale=plane_0[:],
+                start=True,
+                stop=True,
+            )
         groups = [(t, a * HALF, (a + 1) * HALF, "bank_%d_%d" % (a, t)) for a in range(2) for t in range(PACK)][:-1]
         groups = groups + [(3, HALF, 3 * QUARTER, "bank_1_3"), (3, 3 * QUARTER, S, "bank_0_0")]
 

@@ -69,12 +69,11 @@ def tile_picked_dconv_none_e_kernel(tc, xT, w1, w2_words, w2_scales, taps, offs,
                 out=w2_plane[32 * q : 32 * q + 4, :].bitcast(I32), in_=w2_scales[0, 4 * q : 4 * q + 4, :].bitcast(I32)
             )
 
-        OVER = 16
-        early = keep.tile([P, 2 * T - OVER], U32, name="early")
-        pairs = {(0, 0): early[:, 0:T], (0, 1): early[:, T - OVER :]}
-        for u in range(2):
-            window = keep.tile([P, T], U32, name="pairs_1_%d" % u, align_bytes=64)
-            pairs[1, u] = window[:]
+        pairs = {}
+        for c in range(PASSES):
+            for u in range(2):
+                window = keep.tile([P, T], U32, name="pairs_%d_%d" % (c, u), align_bytes=64)
+                pairs[c, u] = window[:]
         picked = [keep.tile([P, 2, S], U32, name="picked_%d" % c) for c in range(PASSES)]
         x_quads, x_plane = {}, {}
         quads = keep.tile([P, S], U32, name="x_quads_1_0", align_bytes=64)
@@ -112,15 +111,15 @@ def tile_picked_dconv_none_e_kernel(tc, xT, w1, w2_words, w2_scales, taps, offs,
             cast_x(scalar_copy, c, u, share, T)
             cast_x(vector_copy, c, u, 0, share)
 
-        cast_shared(0, 0, 672)
+        cast_shared(0, 0, 664)
         gather_whole(0)
-        cast_shared(0, 1, 672)
-        finish_x(0)
-        cast_shared(1, 0, 600)
+        cast_shared(0, 1, 624)
+        nc.vector.tensor_copy(out=picked[0][:, 1, :], in_=pairs[0, 1].indirect(offsets[:]))
+        cast_shared(1, 0, 656)
         gather_whole(1)
         quads_0 = keep.tile([P, S, 2], U32, name="x_quads_0", tag="x_raw_1_0", align_bytes=64)
         nc.scalar.copy(out=quads_0[:], in_=picked[0][:].rearrange("p u n -> p n u"))
-        cast_shared(1, 1, 640)
+        cast_shared(1, 1, 784)
         plane_0 = keep.tile([P, S], U8, name="x_plane_0", tag="x_raw_1_1", align_bytes=64)
         nc.vector.quantize_mx(
             out=x_codes[0][:].bitcast(FP8X4),

@@ -119,7 +119,7 @@ def tile_picked_dconv_none_e_kernel(tc, xT, w1, w2_words, w2_scales, taps, offs,
         gather_whole(1)
         quads_0 = keep.tile([P, S, 2], U32, name="x_quads_0", tag="x_raw_1_0", align_bytes=64)
         nc.scalar.copy(out=quads_0[:], in_=picked[0][:].rearrange("p u n -> p n u"))
-        cast_shared(1, 1, 784)
+        cast_shared(1, 1, 848)
         plane_0 = keep.tile([P, S], U8, name="x_plane_0", tag="x_raw_1_1", align_bytes=64)
         nc.vector.quantize_mx(
             out=x_codes[0][:].bitcast(FP8X4),
@@ -183,7 +183,8 @@ def tile_picked_dconv_none_e_kernel(tc, xT, w1, w2_words, w2_scales, taps, offs,
             for g in range(2):
                 w_bf[c, g] = keep.tile([P, 2, P, PACK], BF16, name="w_bf_%d_%d" % (c, g), align_bytes=64)
         cast_w(scalar_copy, 0, 0, 0, P)
-        quantize_w(0, 0, 2)
+        quantize_w(0, 0, 1)
+        quantize_w(0, 1, 2)
         quantize_x(1, 0, "w_bf_0_0")
         cast_w(scalar_copy, 0, 1, 0, P)
         cast_w(scalar_copy, 1, 0, 86, P)

@@ -83,7 +83,10 @@ def tile_picked_dconv_none_e_kernel(tc, xT, w1, w2_words, w2_scales, taps, offs,
 
         def cast_x(copy, c, u, lo, hi):
             dst = pairs[c, u].bitcast(BF16).rearrange("p (n e) -> p n e", e=2)
-            copy(dst[:, lo:hi, :], x_raw[c, u][:, :, lo:hi].rearrange("p e n -> p n e"))
+            copy(
+                dst[:, lo:hi, :].rearrange("p (c i) e -> p c e i", i=4),
+                x_raw[c, u][:, :, lo:hi].rearrange("p e (c i) -> p c e i", i=4),
+            )
 
         def gather_whole(c):
             nc.vector.tensor_copy(out=picked[c][:, 0, :], in_=pairs[c, 0].indirect(offsets[:]))
@@ -95,8 +98,8 @@ def tile_picked_dconv_none_e_kernel(tc, xT, w1, w2_words, w2_scales, taps, offs,
 
         def weave_x(c, a):
             nc.vector.tensor_copy(
-                out=x_quads[c, a].bitcast(I32).rearrange("p (n u) -> p n u", u=2),
-                in_=picked[c][:, :, halves[a]].bitcast(I32).rearrange("p u n -> p n u"),
+                out=x_quads[c, a].bitcast(I32).rearrange("p (c i u) -> p c u i", u=2, i=4),
+                in_=picked[c][:, :, halves[a]].bitcast(I32).rearrange("p u (c i) -> p c u i", i=4),
             )
 
         def quantize_x(c, a, tag):
@@ -118,7 +121,10 @@ def tile_picked_dconv_none_e_kernel(tc, xT, w1, w2_words, w2_scales, taps, offs,
         cast_shared(1, 0, 656)
         gather_whole(1)
         quads_0 = keep.tile([P, S, 2], U32, name="x_quads_0", tag="x_raw_1_0", align_bytes=64)
-        nc.scalar.copy(out=quads_0[:], in_=picked[0][:].rearrange("p u n -> p n u"))
+        nc.scalar.copy(
+            out=quads_0[:].rearrange("p (c i) u -> p c u i", i=4),
+            in_=picked[0][:].rearrange("p u (c i) -> p c u i", i=4),
+        )
         cast_shared(1, 1, 848)
         plane_0 = keep.tile([P, S], U8, name="x_plane_0", tag="x_raw_1_1", align_bytes=64)
         nc.vector.quantize_mx(
@@ -199,8 +205,8 @@ def tile_picked_dconv_none_e_kernel(tc, xT, w1, w2_words, w2_scales, taps, offs,
         last_quads = stage.tile([P, S], U32, name="x_quads_1_1", align_bytes=64, offset=8192)
         x_quads[1, 1] = last_quads[:]
         nc.scalar.copy(
-            out=last_quads[:].rearrange("p (n u) -> p n u", u=2),
-            in_=picked[1][:, :, halves[1]].rearrange("p u n -> p n u"),
+            out=last_quads[:].rearrange("p (c i u) -> p c u i", u=2, i=4),
+            in_=picked[1][:, :, halves[1]].rearrange("p u (c i) -> p c u i", i=4),
         )
         quantize_x(1, 1, "x_plane_1_1")
 

@@ -275,5 +275,6 @@ def tile_picked_dconv_none_e_kernel(tc, xT, w1, w2_words, w2_scales, taps, offs,
         quantize_z(3)
         quantize_z(2)
         second_product(vector_copy, 3 * QUARTER, S, "bank_0_1")
+        nc.sync.dma_start(out=out[:, 3 * QUARTER : S], in_=result[1][:, QUARTER:HALF])
         second_product(vector_copy, HALF, 3 * QUARTER, "bank_0_2")
-        nc.sync.dma_start(out=out[:, HALF:S], in_=result[1][:])
+        nc.sync.dma_start(out=out[:, HALF : 3 * QUARTER], in_=result[1][:, 0:QUARTER])

@@ -91,10 +91,9 @@ def tile_picked_dconv_none_e_kernel(tc, xT, w1, w2_words, w2_scales, taps, offs,
         def gather_whole(c):
             nc.vector.tensor_copy(out=picked[c][:, 0, :], in_=pairs[c, 0].indirect(offsets[:]))
 
-        def finish_x(c):
-            for a, tokens in enumerate(halves):
-                entries = offsets[:, a * HALF // 16 : (a + 1) * HALF // 16]
-                nc.vector.tensor_copy(out=picked[c][:, 1, tokens], in_=pairs[c, 1].indirect(entries))
+        def gather_half(c, a):
+            entries = offsets[:, a * HALF // 16 : (a + 1) * HALF // 16]
+            nc.vector.tensor_copy(out=picked[c][:, 1, halves[a]], in_=pairs[c, 1].indirect(entries))
 
         def weave_x(c, a):
             nc.vector.tensor_copy(
@@ -126,6 +125,7 @@ def tile_picked_dconv_none_e_kernel(tc, xT, w1, w2_words, w2_scales, taps, offs,
             in_=picked[0][:].rearrange("p u (c i) -> p c u i", i=4),
         )
         cast_shared(1, 1, 848)
+        gather_half(1, 0)
         plane_0 = keep.tile([P, S], U8, name="x_plane_0", tag="x_raw_1_1", align_bytes=64)
         nc.vector.quantize_mx(
             out=x_codes[0][:].bitcast(FP8X4),
@@ -134,7 +134,7 @@ def tile_picked_dconv_none_e_kernel(tc, xT, w1, w2_words, w2_scales, taps, offs,
         )
         for a in range(2):
             x_plane[0, a] = plane_0[:, halves[a]]
-        finish_x(1)
+        gather_half(1, 1)
         weave_x(1, 0)
 
         w_codes = [keep.tile([P, H], U32, name="w_codes_%d" % c, align_bytes=64) for c in range(PASSES)]

@@ -48,12 +48,14 @@ def tile_picked_dconv_none_e_kernel(tc, xT, w1, w2_words, w2_scales, taps, offs,
         nc.vector.memset(w2_plane[:].bitcast(I32), 0)
         nc.vector.memset(delayed[:, :, 0:1], 0.0)
 
-        x_raw = {}
+        x_raw, x_flat = {}, {}
         for c in range(PASSES):
             rows = xT[c * K_PASS : (c + 1) * K_PASS, :].rearrange("(p u e) n -> p u e n", u=2, e=2)
             for u in range(2):
-                x_raw[c, u] = keep.tile([P, 2, T], F32, name="x_raw_%d_%d" % (c, u), align_bytes=64)
-                nc.sync.dma_start(out=x_raw[c, u][:], in_=rows[:, u, :, :])
+                room = 2 * S - 16 if (c, u) == (1, 0) else 0
+                x_flat[c, u] = keep.tile([P, 2 * T + room], F32, name="x_raw_%d_%d" % (c, u), align_bytes=64)
+                x_raw[c, u] = x_flat[c, u][:, 0 : 2 * T].rearrange("p (e n) -> p e n", e=2)
+                nc.sync.dma_start(out=x_raw[c, u], in_=rows[:, u, :, :])
                 if c == 0 and u == 0:
                     nc.sync.dma_start(offsets[:], offs)
         w_raw = []
@@ -117,25 +119,24 @@ def tile_picked_dconv_none_e_kernel(tc, xT, w1, w2_words, w2_scales, taps, offs,
         gather_whole(0)
         cast_shared(0, 1, 624)
         nc.vector.tensor_copy(out=picked[0][:, 1, :], in_=pairs[0, 1].indirect(offsets[:]))
-        cast_shared(1, 0, 656)
+        cast_x(scalar_copy, 1, 0, 840, T)
+        cast_x(scalar_copy, 1, 0, 656, 840)
+        cast_x(vector_copy, 1, 0, 0, 656)
         gather_whole(1)
-        quads_0 = keep.tile([P, S, 2], U32, name="x_quads_0", tag="x_raw_1_0", align_bytes=64)
+        quads_0 = x_flat[1, 0][:, 2 * T - 16 : 2 * T - 16 + 2 * S].bitcast(U32)
         nc.scalar.copy(
-            out=quads_0[:].rearrange("p (c i) u -> p c u i", i=4),
+            out=quads_0.rearrange("p (c i u) -> p c u i", u=2, i=4),
             in_=picked[0][:].rearrange("p u (c i) -> p c u i", i=4),
         )
-        cast_shared(1, 1, 848)
+        cast_shared(1, 1, 688)
         gather_half(1, 0)
         plane_0 = keep.tile([P, S], U8, name="x_plane_0", tag="x_raw_1_1", align_bytes=64)
-        nc.vector.quantize_mx(
-            out=x_codes[0][:].bitcast(FP8X4),
-            scales=plane_0[:],
-            in_=quads_0[:].rearrange("p n u -> p (n u)").bitcast(BF16),
-        )
+        nc.vector.quantize_mx(out=x_codes[0][:].bitcast(FP8X4), scales=plane_0[:], in_=quads_0.bitcast(BF16))
         for a in range(2):
             x_plane[0, a] = plane_0[:, halves[a]]
-        gather_half(1, 1)
         weave_x(1, 0)
+        gather_half(1, 1)
+        quantize_x(1, 0, "x_plane_1_0")
 
         w_codes = [keep.tile([P, H], U32, name="w_codes_%d" % c, align_bytes=64) for c in range(PASSES)]
         w_bf, w_plane = {}, {}
@@ -155,16 +156,19 @@ def tile_picked_dconv_none_e_kernel(tc, xT, w1, w2_words, w2_scales, taps, offs,
             )
 
         warm = psum.tile([P, S], F32, name="warm", tag="bank_1_3")
-        for turn in range(2):
+
+        def warm_up(codes, plane, width):
             nc.tensor.matmul_mx(
-                out=warm[:],
-                lhsT=x_codes[0][:, 0:P].bitcast(FP8X4),
-                lhsT_scale=plane_0[:, 0:P],
-                rhs=x_codes[0][:].bitcast(FP8X4),
-                rhs_scale=plane_0[:],
+                out=warm[:, 0:width],
+                lhsT=codes.bitcast(FP8X4),
+                lhsT_scale=plane,
+                rhs=x_codes[0][:, 0:width].bitcast(FP8X4),
+                rhs_scale=plane_0[:, 0:width],
                 start=True,
                 stop=True,
             )
+
+        warm_up(x_codes[0][:, 0:P], plane_0[:, 0:P], S)
         groups = [(t, a * HALF, (a + 1) * HALF, "bank_%d_%d" % (a, t)) for a in range(2) for t in range(PACK)][:-1]
         groups = groups + [(3, HALF, 3 * QUARTER, "bank_1_3"), (3, 3 * QUARTER, S, "bank_0_0")]
 
@@ -191,7 +195,12 @@ def tile_picked_dconv_none_e_kernel(tc, xT, w1, w2_words, w2_scales, taps, offs,
         cast_w(scalar_copy, 0, 0, 0, P)
         quantize_w(0, 0, 1)
         quantize_w(0, 1, 2)
-        quantize_x(1, 0, "w_bf_0_0")
+        banks = {}
+        for t, lo, hi, bank in groups:
+            if t < 2:
+                banks[t, lo] = psum.tile([P, hi - lo], F32, name="h_%d_%d" % (t, lo), tag=bank)
+                first_product(banks[t, lo], 0, t, lo, hi, True)
+        warm_up(w_codes[0][:, P : 2 * P], w_plane[0, 0][:, P : 2 * P], HALF)
         cast_w(scalar_copy, 0, 1, 0, P)
         cast_w(scalar_copy, 1, 0, 86, P)
         cast_w(vector_copy, 1, 0, 0, 86)
@@ -215,10 +224,13 @@ def tile_picked_dconv_none_e_kernel(tc, xT, w1, w2_words, w2_scales, taps, offs,
         z_codes = keep.tile([P, S], U32, name="z_codes", align_bytes=64)
         z_plane = keep.tile([P, S], U8, name="z_plane", align_bytes=64)
         for t, lo, hi, bank in groups:
-            h = psum.tile([P, hi - lo], F32, name="h_%d_%d" % (t, lo), tag=bank)
-            order = (1, 0) if t >= 2 else (0, 1)
-            first_product(h, order[0], t, lo, hi, True)
-            first_product(h, order[1], t, lo, hi, False)
+            if t < 2:
+                h = banks[t, lo]
+                first_product(h, 1, t, lo, hi, False)
+            else:
+                h = psum.tile([P, hi - lo], F32, name="h_%d_%d" % (t, lo), tag=bank)
+                first_product(h, 1, t, lo, hi, True)
+                first_product(h, 0, t, lo, hi, False)
             nc.scalar.activation(out=delayed[:, t, lo + 1 : hi + 1], in_=h[:], func=COPY, scale=tap[:, t, 1:2])
             nc.vector.scalar_tensor_tensor(
                 out=z_rows[lo // HALF][:, t, lo % HALF : lo % HALF + hi - lo],

@@ -168,7 +168,8 @@ def tile_picked_dconv_none_e_kernel(tc, xT, w1, w2_words, w2_scales, taps, offs,
                 stop=True,
             )
 
-        warm_up(x_codes[0][:, 0:P], plane_0[:, 0:P], S)
+        for turn in range(2):
+            warm_up(x_codes[0][:, 0:P], plane_0[:, 0:P], S)
         groups = [(t, a * HALF, (a + 1) * HALF, "bank_%d_%d" % (a, t)) for a in range(2) for t in range(PACK)][:-1]
         groups = groups + [(3, HALF, 3 * QUARTER, "bank_1_3"), (3, 3 * QUARTER, S, "bank_0_0")]
 
@@ -200,7 +201,6 @@ def tile_picked_dconv_none_e_kernel(tc, xT, w1, w2_words, w2_scales, taps, offs,
             if t < 2:
                 banks[t, lo] = psum.tile([P, hi - lo], F32, name="h_%d_%d" % (t, lo), tag=bank)
                 first_product(banks[t, lo], 0, t, lo, hi, True)
-        warm_up(w_codes[0][:, P : 2 * P], w_plane[0, 0][:, P : 2 * P], HALF)
         cast_w(scalar_copy, 0, 1, 0, P)
         cast_w(scalar_copy, 1, 0, 86, P)
         cast_w(vector_copy, 1, 0, 0, 86)

@@ -46,24 +46,30 @@ def tile_picked_dconv_none_e_kernel(tc, xT, w1, w2_words, w2_scales, taps, offs,
         delayed = keep.tile([P, PACK, S + 8], F32, name="delayed")
 
         nc.vector.memset(w2_plane[:].bitcast(I32), 0)
-        nc.vector.memset(delayed[:, :, 0:1], 0.0)
+        zero = keep.tile([P, PACK, 1], F32, name="zero")
+        nc.vector.memset(zero[:], 0.0)
+        scalar_copy(delayed[:, :, 0:1], zero[:])
 
-        x_raw, x_flat = {}, {}
-        for c in range(PASSES):
-            rows = xT[c * K_PASS : (c + 1) * K_PASS, :].rearrange("(p u e) n -> p u e n", u=2, e=2)
-            for u in range(2):
-                room = 2 * S - 16 if (c, u) == (1, 0) else 0
-                x_flat[c, u] = keep.tile([P, 2 * T + room], F32, name="x_raw_%d_%d" % (c, u), align_bytes=64)
-                x_raw[c, u] = x_flat[c, u][:, 0 : 2 * T].rearrange("p (e n) -> p e n", e=2)
-                nc.sync.dma_start(out=x_raw[c, u], in_=rows[:, u, :, :])
-                if c == 0 and u == 0:
-                    nc.sync.dma_start(offsets[:], offs)
-        w_raw = []
-        for c in range(PASSES):
-            w_raw.append(stage.tile([P, PACK, H], F32, name="w_raw_%d" % c, align_bytes=64, offset=8192 * c))
+        x_raw, w_raw = {}, {}
+
+        def load_x(c, u):
+            rows = xT[c * K_PASS : (c + 1) * K_PASS, :].rearrange("(p u e) n -> p u (e n)", u=2, e=2)
+            x_raw[c, u] = keep.tile([P, 2 * T], F32, name="x_raw_%d_%d" % (c, u), align_bytes=64)
+            nc.sync.dma_start(out=x_raw[c, u][:], in_=rows[:, u, :])
+
+        def load_w(c):
+            w_raw[c] = keep.tile([P, PACK, H], F32, name="w_raw_%d" % c, align_bytes=64)
             nc.sync.dma_start(
                 out=w_raw[c][:], in_=w1[c * K_PASS : (c + 1) * K_PASS, :].rearrange("(p j) n -> p j n", j=PACK)
             )
+
+        load_x(0, 0)
+        nc.sync.dma_start(offsets[:], offs)
+        load_x(0, 1)
+        load_x(1, 0)
+        load_w(0)
+        load_x(1, 1)
+        load_w(1)
         nc.sync.dma_start(out=tap[:], in_=taps.rearrange("(p t) d -> p t d", t=PACK))
         nc.sync.dma_start(out=w2_codes[:].bitcast(I32), in_=w2_words[0].bitcast(I32))
         for q in range(4):
@@ -71,75 +77,57 @@ def tile_picked_dconv_none_e_kernel(tc, xT, w1, w2_words, w2_scales, taps, offs,
                 out=w2_plane[32 * q : 32 * q + 4, :].bitcast(I32), in_=w2_scales[0, 4 * q : 4 * q + 4, :].bitcast(I32)
             )
 
-        pairs = {}
-        for c in range(PASSES):
-            for u in range(2):
-                window = keep.tile([P, T], U32, name="pairs_%d_%d" % (c, u), align_bytes=64)
-                pairs[c, u] = window[:]
-        picked = [keep.tile([P, 2, S], U32, name="picked_%d" % c) for c in range(PASSES)]
-        x_quads, x_plane = {}, {}
-        quads = keep.tile([P, S], U32, name="x_quads_1_0", align_bytes=64)
-        x_quads[1, 0] = quads[:]
-        x_codes = [keep.tile([P, S], U32, name="x_codes_%d" % c, align_bytes=64) for c in range(PASSES)]
         halves = [slice(a * HALF, (a + 1) * HALF) for a in range(2)]
+        x_codes = [keep.tile([P, S], U32, name="x_codes_%d" % c, align_bytes=64) for c in range(PASSES)]
+        x_plane = {}
 
-        def cast_x(copy, c, u, lo, hi):
-            dst = pairs[c, u].bitcast(BF16).rearrange("p (n e) -> p n e", e=2)
+        def gather(copy, dst, c, j, lo, hi):
+            window = x_raw[c, j // 2][:, (j % 2) * T : (j % 2 + 1) * T]
+            copy(dst, window.indirect(offsets[:, lo // 16 : hi // 16]))
+
+        def weave(copy, quads, picked, j0, j1, lo, hi):
             copy(
-                dst[:, lo:hi, :].rearrange("p (c i) e -> p c e i", i=4),
-                x_raw[c, u][:, :, lo:hi].rearrange("p e (c i) -> p c e i", i=4),
+                quads[:].rearrange("p (c i j) -> p c j i", i=4, j=PACK)[:, lo // 4 : hi // 4, j0:j1, :],
+                picked[:].rearrange("p j (c i) -> p c j i", i=4)[:, lo // 4 : hi // 4, j0:j1, :],
             )
 
-        def gather_whole(c):
-            nc.vector.tensor_copy(out=picked[c][:, 0, :], in_=pairs[c, 0].indirect(offsets[:]))
+        picked_0 = keep.tile([P, PACK, S], F32, name="picked_0")
+        for j in range(PACK):
+            gather(vector_copy if j % 2 else scalar_copy, picked_0[:, j, :], 0, j, 0, S)
+        quads_0 = keep.tile([P, S * PACK], BF16, name="quads_0", align_bytes=64)
+        weave(scalar_copy, quads_0, picked_0, 0, PACK, 336, S)
+        weave(vector_copy, quads_0, picked_0, 0, PACK, 0, 336)
+        early = keep.tile([P, 2, S], F32, name="picked_1_early")
+        late = [keep.tile([P, 2, HALF], F32, name="picked_1_late_%d" % a) for a in range(2)]
+        quads_1 = [keep.tile([P, HALF * PACK], BF16, name="quads_1_%d" % a, align_bytes=64) for a in range(2)]
 
-        def gather_half(c, a):
-            entries = offsets[:, a * HALF // 16 : (a + 1) * HALF // 16]
-            nc.vector.tensor_copy(out=picked[c][:, 1, halves[a]], in_=pairs[c, 1].indirect(entries))
-
-        def weave_x(c, a):
-            nc.vector.tensor_copy(
-                out=x_quads[c, a].bitcast(I32).rearrange("p (c i u) -> p c u i", u=2, i=4),
-                in_=picked[c][:, :, halves[a]].bitcast(I32).rearrange("p u (c i) -> p c u i", i=4),
+        def weave_pair(copy, a, u, src, lo=0, hi=HALF):
+            copy(
+                quads_1[a][:].rearrange("p (c i j) -> p c j i", i=4, j=PACK)[:, lo // 4 : hi // 4, 2 * u : 2 * u + 2, :],
+                src.rearrange("p j (c i) -> p c j i", i=4)[:, lo // 4 : hi // 4, :, :],
             )
 
-        def quantize_x(c, a, tag):
-            x_plane[c, a] = keep.tile([P, HALF], U8, name="x_plane_%d_%d" % (c, a), tag=tag, align_bytes=64)
-            nc.vector.quantize_mx(
-                out=x_codes[c][:, halves[a]].bitcast(FP8X4),
-                scales=x_plane[c, a][:],
-                in_=x_quads[c, a].bitcast(BF16),
-            )
+        def quantize_x(a, tag):
+            plane = keep.tile([P, HALF], U8, name="x_plane_1_%d" % a, tag=tag, align_bytes=64)
+            x_plane[1, a] = plane[:]
+            nc.vector.quantize_mx(out=x_codes[1][:, halves[a]].bitcast(FP8X4), scales=plane[:], in_=quads_1[a][:])
 
-        def cast_shared(c, u, share):
-            cast_x(scalar_copy, c, u, share, T)
-            cast_x(vector_copy, c, u, 0, share)
-
-        cast_shared(0, 0, 664)
-        gather_whole(0)
-        cast_shared(0, 1, 624)
-        nc.vector.tensor_copy(out=picked[0][:, 1, :], in_=pairs[0, 1].indirect(offsets[:]))
-        cast_x(scalar_copy, 1, 0, 840, T)
-        cast_x(scalar_copy, 1, 0, 656, 840)
-        cast_x(vector_copy, 1, 0, 0, 656)
-        gather_whole(1)
-        quads_0 = x_flat[1, 0][:, 2 * T - 16 : 2 * T - 16 + 2 * S].bitcast(U32)
-        nc.scalar.copy(
-            out=quads_0.rearrange("p (c i u) -> p c u i", u=2, i=4),
-            in_=picked[0][:].rearrange("p u (c i) -> p c u i", i=4),
-        )
-        cast_shared(1, 1, 688)
-        gather_half(1, 0)
-        plane_0 = keep.tile([P, S], U8, name="x_plane_0", tag="x_raw_1_1", align_bytes=64)
-        nc.vector.quantize_mx(out=x_codes[0][:].bitcast(FP8X4), scales=plane_0[:], in_=quads_0.bitcast(BF16))
+        gather(scalar_copy, early[:, 0, :], 1, 0, 0, S)
+        gather(vector_copy, early[:, 1, :], 1, 1, 0, S)
+        plane_0 = keep.tile([P, S], U8, name="x_plane_0", tag="x_raw_1_0", align_bytes=64)
         for a in range(2):
             x_plane[0, a] = plane_0[:, halves[a]]
-        weave_x(1, 0)
-        gather_half(1, 1)
-        quantize_x(1, 0, "x_plane_1_0")
+        nc.vector.quantize_mx(out=x_codes[0][:].bitcast(FP8X4), scales=plane_0[:], in_=quads_0[:])
+        weave_pair(scalar_copy, 1, 0, early[:, :, halves[1]])
+        weave_pair(vector_copy, 0, 0, early[:, :, halves[0]])
 
         w_codes = [keep.tile([P, H], U32, name="w_codes_%d" % c, align_bytes=64) for c in range(PASSES)]
         w_bf, w_plane = {}, {}
+        for c in range(PASSES):
+            for g in range(2):
+                w_bf[c, g] = keep.tile([P, 2, P, PACK], BF16, name="w_bf_%d_%d" % (c, g), align_bytes=64)
+                plane = keep.tile([P, H // 2], U8, name="w_plane_%d_%d" % (c, g), align_bytes=64)
+                w_plane[c, g] = plane[:]
 
         def cast_w(copy, c, g, m0, m1):
             copy(
@@ -155,23 +143,7 @@ def tile_picked_dconv_none_e_kernel(tc, xT, w1, w2_words, w2_scales, taps, offs,
                 in_=w_bf[c, t0 // 2][:, t0 % 2 : t0 % 2 + t1 - t0, :, :].rearrange("p t m j -> p (t m j)"),
             )
 
-        warm = psum.tile([P, S], F32, name="warm", tag="bank_1_3")
-
-        def warm_up(codes, plane, width):
-            nc.tensor.matmul_mx(
-                out=warm[:, 0:width],
-                lhsT=codes.bitcast(FP8X4),
-                lhsT_scale=plane,
-                rhs=x_codes[0][:, 0:width].bitcast(FP8X4),
-                rhs_scale=plane_0[:, 0:width],
-                start=True,
-                stop=True,
-            )
-
-        for turn in range(2):
-            warm_up(x_codes[0][:, 0:P], plane_0[:, 0:P], S)
-        groups = [(t, a * HALF, (a + 1) * HALF, "bank_%d_%d" % (a, t)) for a in range(2) for t in range(PACK)][:-1]
-        groups = groups + [(3, HALF, 3 * QUARTER, "bank_1_3"), (3, 3 * QUARTER, S, "bank_0_0")]
+        groups = [(t, a * HALF, (a + 1) * HALF, "bank_%d_%d" % (a, t)) for a in range(2) for t in range(PACK)]
 
         def first_product(acc, c, t, lo, hi, first):
             cols = slice(t * P, (t + 1) * P)
@@ -185,52 +157,36 @@ def tile_picked_dconv_none_e_kernel(tc, xT, w1, w2_words, w2_scales, taps, offs,
                 stop=not first,
             )
 
-        for c, g in ((0, 0), (1, 0), (1, 1)):
-            plane = keep.tile([P, H // 2], U8, name="w_plane_%d_%d" % (c, g), align_bytes=64)
-            w_plane[c, g] = plane[:]
-        plane = stage.tile([P, H // 2], U8, name="w_plane_0_1", align_bytes=64, offset=12288)
-        w_plane[0, 1] = plane[:]
-        for c in range(PASSES):
-            for g in range(2):
-                w_bf[c, g] = keep.tile([P, 2, P, PACK], BF16, name="w_bf_%d_%d" % (c, g), align_bytes=64)
-        cast_w(scalar_copy, 0, 0, 0, P)
-        quantize_w(0, 0, 1)
-        quantize_w(0, 1, 2)
+        for g in range(2):
+            cast_w(scalar_copy, 0, g, 60, P)
+            cast_w(vector_copy, 0, g, 0, 60)
+            quantize_w(0, 2 * g, 2 * g + 2)
         banks = {}
         for t, lo, hi, bank in groups:
-            if t < 2:
-                banks[t, lo] = psum.tile([P, hi - lo], F32, name="h_%d_%d" % (t, lo), tag=bank)
-                first_product(banks[t, lo], 0, t, lo, hi, True)
-        cast_w(scalar_copy, 0, 1, 0, P)
+            banks[t, lo] = psum.tile([P, hi - lo], F32, name="h_%d_%d" % (t, lo), tag=bank)
+            first_product(banks[t, lo], 0, t, lo, hi, True)
+        for a in range(2):
+            gather(scalar_copy, late[a][:, 0, :], 1, 2, a * HALF, (a + 1) * HALF)
+            gather(vector_copy, late[a][:, 1, :], 1, 3, a * HALF, (a + 1) * HALF)
+        weave_pair(vector_copy, 0, 1, late[0][:])
+        weave_pair(vector_copy, 1, 1, late[1][:], 0, 64)
+        weave_pair(scalar_copy, 1, 1, late[1][:], 64, HALF)
+        quantize_x(0, "x_plane_1_0")
         cast_w(scalar_copy, 1, 0, 86, P)
         cast_w(vector_copy, 1, 0, 0, 86)
-        cast_w(scalar_copy, 1, 1, 78, P)
-        cast_w(vector_copy, 1, 1, 0, 78)
-        quantize_w(1, 0, 1)
-        quantize_w(1, 1, 2)
-        quantize_w(0, 2, 4)
-        quantize_w(1, 2, 3)
-        quantize_w(1, 3, 4)
-        last_quads = stage.tile([P, S], U32, name="x_quads_1_1", align_bytes=64, offset=8192)
-        x_quads[1, 1] = last_quads[:]
-        nc.scalar.copy(
-            out=last_quads[:].rearrange("p (c i u) -> p c u i", u=2, i=4),
-            in_=picked[1][:, :, halves[1]].rearrange("p u (c i) -> p c u i", i=4),
-        )
-        quantize_x(1, 1, "x_plane_1_1")
+        cast_w(scalar_copy, 1, 1, 76, P)
+        cast_w(vector_copy, 1, 1, 0, 76)
+        for t in range(PACK):
+            quantize_w(1, t, t + 1)
+        quantize_x(1, "w_bf_1_0")
 
         z_rows = [keep.tile([P, PACK, HALF], F32, name="z_rows_%d" % a) for a in range(2)]
         z_bf = keep.tile([P, S * PACK], BF16, name="z_bf", align_bytes=64)
         z_codes = keep.tile([P, S], U32, name="z_codes", align_bytes=64)
         z_plane = keep.tile([P, S], U8, name="z_plane", align_bytes=64)
         for t, lo, hi, bank in groups:
-            if t < 2:
-                h = banks[t, lo]
-                first_product(h, 1, t, lo, hi, False)
-            else:
-                h = psum.tile([P, hi - lo], F32, name="h_%d_%d" % (t, lo), tag=bank)
-                first_product(h, 1, t, lo, hi, True)
-                first_product(h, 0, t, lo, hi, False)
+            h = banks[t, lo]
+            first_product(h, 1, t, lo, hi, False)
             nc.scalar.activation(out=delayed[:, t, lo + 1 : hi + 1], in_=h[:], func=COPY, scale=tap[:, t, 1:2])
             nc.vector.scalar_tensor_tensor(
                 out=z_rows[lo // HALF][:, t, lo % HALF : lo % HALF + hi - lo],

@@ -52,10 +52,12 @@ def tile_picked_dconv_none_e_kernel(tc, xT, w1, w2_words, w2_scales, taps, offs,
 
         x_raw, w_raw = {}, {}
 
-        def load_x(c, u):
-            rows = xT[c * K_PASS : (c + 1) * K_PASS, :].rearrange("(p u e) n -> p u (e n)", u=2, e=2)
-            x_raw[c, u] = keep.tile([P, 2 * T], F32, name="x_raw_%d_%d" % (c, u), align_bytes=64)
-            nc.sync.dma_start(out=x_raw[c, u][:], in_=rows[:, u, :])
+        def load_x(c, j0, j1):
+            rows = xT[c * K_PASS : (c + 1) * K_PASS, :].rearrange("(p j) n -> p (j n)", j=PACK)
+            raw = keep.tile([P, (j1 - j0) * T], F32, name="x_raw_%d_%d" % (c, j0), align_bytes=64)
+            nc.sync.dma_start(out=raw[:], in_=rows[:, j0 * T : j1 * T])
+            for j in range(j0, j1):
+                x_raw[c, j] = raw[:, (j - j0) * T : (j - j0 + 1) * T]
 
         def load_w(c):
             w_raw[c] = keep.tile([P, PACK, H], F32, name="w_raw_%d" % c, align_bytes=64)
@@ -63,12 +65,13 @@ def tile_picked_dconv_none_e_kernel(tc, xT, w1, w2_words, w2_scales, taps, offs,
                 out=w_raw[c][:], in_=w1[c * K_PASS : (c + 1) * K_PASS, :].rearrange("(p j) n -> p j n", j=PACK)
             )
 
-        load_x(0, 0)
+        load_x(0, 0, 2)
         nc.sync.dma_start(offsets[:], offs)
-        load_x(0, 1)
-        load_x(1, 0)
+        load_x(0, 2, 4)
+        load_x(1, 0, 2)
+        load_x(1, 2, 3)
         load_w(0)
-        load_x(1, 1)
+        load_x(1, 3, 4)
         load_w(1)
         nc.sync.dma_start(out=tap[:], in_=taps.rearrange("(p t) d -> p t d", t=PACK))
         nc.sync.dma_start(out=w2_codes[:].bitcast(I32), in_=w2_words[0].bitcast(I32))
@@ -82,8 +85,7 @@ def tile_picked_dconv_none_e_kernel(tc, xT, w1, w2_words, w2_scales, taps, offs,
         x_plane = {}
 
         def gather(copy, dst, c, j, lo, hi):
-            window = x_raw[c, j // 2][:, (j % 2) * T : (j % 2 + 1) * T]
-            copy(dst, window.indirect(offsets[:, lo // 16 : hi // 16]))
+            copy(dst, x_raw[c, j].indirect(offsets[:, lo // 16 : hi // 16]))
 
         def weave(copy, quads, picked, j0, j1, lo, hi):
             copy(
@@ -95,16 +97,20 @@ def tile_picked_dconv_none_e_kernel(tc, xT, w1, w2_words, w2_scales, taps, offs,
         for j in range(PACK):
             gather(vector_copy if j % 2 else scalar_copy, picked_0[:, j, :], 0, j, 0, S)
         quads_0 = keep.tile([P, S * PACK], BF16, name="quads_0", align_bytes=64)
-        weave(scalar_copy, quads_0, picked_0, 0, PACK, 336, S)
-        weave(vector_copy, quads_0, picked_0, 0, PACK, 0, 336)
-        early = keep.tile([P, 2, S], F32, name="picked_1_early")
-        late = [keep.tile([P, 2, HALF], F32, name="picked_1_late_%d" % a) for a in range(2)]
+        weave(vector_copy, quads_0, picked_0, 0, PACK, 0, S)
+        picked_1 = {}
+        for u in range(2):
+            for a in range(2):
+                picked_1[u, a] = keep.tile([P, 2, HALF], F32, name="picked_1_%d_%d" % (u, a))
         quads_1 = [keep.tile([P, HALF * PACK], BF16, name="quads_1_%d" % a, align_bytes=64) for a in range(2)]
 
-        def weave_pair(copy, a, u, src, lo=0, hi=HALF):
-            copy(
-                quads_1[a][:].rearrange("p (c i j) -> p c j i", i=4, j=PACK)[:, lo // 4 : hi // 4, 2 * u : 2 * u + 2, :],
-                src.rearrange("p j (c i) -> p c j i", i=4)[:, lo // 4 : hi // 4, :, :],
+        def gather_half(j, a):
+            gather(scalar_copy, picked_1[j // 2, a][:, j % 2, :], 1, j, a * HALF, (a + 1) * HALF)
+
+        def weave_pair(u, a):
+            vector_copy(
+                quads_1[a][:].rearrange("p (c i j) -> p c j i", i=4, j=PACK)[:, :, 2 * u : 2 * u + 2, :],
+                picked_1[u, a][:].rearrange("p j (c i) -> p c j i", i=4),
             )
 
         def quantize_x(a, tag):
@@ -112,14 +118,16 @@ def tile_picked_dconv_none_e_kernel(tc, xT, w1, w2_words, w2_scales, taps, offs,
             x_plane[1, a] = plane[:]
             nc.vector.quantize_mx(out=x_codes[1][:, halves[a]].bitcast(FP8X4), scales=plane[:], in_=quads_1[a][:])
 
-        gather(scalar_copy, early[:, 0, :], 1, 0, 0, S)
-        gather(vector_copy, early[:, 1, :], 1, 1, 0, S)
-        plane_0 = keep.tile([P, S], U8, name="x_plane_0", tag="x_raw_1_0", align_bytes=64)
+        plane_0 = keep.tile([P, S], U8, name="x_plane_0", align_bytes=64)
         for a in range(2):
             x_plane[0, a] = plane_0[:, halves[a]]
         nc.vector.quantize_mx(out=x_codes[0][:].bitcast(FP8X4), scales=plane_0[:], in_=quads_0[:])
-        weave_pair(scalar_copy, 1, 0, early[:, :, halves[1]])
-        weave_pair(vector_copy, 0, 0, early[:, :, halves[0]])
+        for a in range(2):
+            gather_half(0, a)
+            gather_half(1, a)
+            weave_pair(0, a)
+        for a in range(2):
+            gather_half(2, a)
 
         w_codes = [keep.tile([P, H], U32, name="w_codes_%d" % c, align_bytes=64) for c in range(PASSES)]
         w_bf, w_plane = {}, {}
@@ -143,7 +151,8 @@ def tile_picked_dconv_none_e_kernel(tc, xT, w1, w2_words, w2_scales, taps, offs,
                 in_=w_bf[c, t0 // 2][:, t0 % 2 : t0 % 2 + t1 - t0, :, :].rearrange("p t m j -> p (t m j)"),
             )
 
-        groups = [(t, a * HALF, (a + 1) * HALF, "bank_%d_%d" % (a, t)) for a in range(2) for t in range(PACK)]
+        groups = [(t, a * HALF, (a + 1) * HALF, "bank_%d_%d" % (a, t)) for a in range(2) for t in range(PACK)][:-1]
+        groups = groups + [(3, HALF, 3 * QUARTER, "bank_1_3"), (3, 3 * QUARTER, S, "bank_0_0")]
 
         def first_product(acc, c, t, lo, hi, first):
             cols = slice(t * P, (t + 1) * P)
@@ -157,20 +166,36 @@ def tile_picked_dconv_none_e_kernel(tc, xT, w1, w2_words, w2_scales, taps, offs,
                 stop=not first,
             )
 
-        for g in range(2):
-            cast_w(scalar_copy, 0, g, 60, P)
-            cast_w(vector_copy, 0, g, 0, 60)
-            quantize_w(0, 2 * g, 2 * g + 2)
         banks = {}
-        for t, lo, hi, bank in groups:
-            banks[t, lo] = psum.tile([P, hi - lo], F32, name="h_%d_%d" % (t, lo), tag=bank)
-            first_product(banks[t, lo], 0, t, lo, hi, True)
+
+        def open_groups(g):
+            for t, lo, hi, bank in groups[:-1]:
+                if t // 2 == g:
+                    banks[t, lo] = psum.tile([P, hi - lo], F32, name="h_%d_%d" % (t, lo), tag=bank)
+                    first_product(banks[t, lo], 0, t, lo, hi, True)
+
+        cast_w(vector_copy, 0, 0, 0, P)
+        cast_w(scalar_copy, 0, 1, 92, P)
+        cast_w(vector_copy, 0, 1, 0, 92)
+        quantize_w(0, 0, 1)
+        quantize_w(0, 1, 2)
+        warm = psum.tile([P, S], F32, name="warm", tag="bank_1_3")
+        for lo, hi in ((0, HALF), (HALF, 3 * QUARTER)):
+            nc.tensor.matmul_mx(
+                out=warm[:, lo:hi],
+                lhsT=w_codes[0][:, 0:P].bitcast(FP8X4),
+                lhsT_scale=w_plane[0, 0][:, 0:P],
+                rhs=x_codes[0][:, lo:hi].bitcast(FP8X4),
+                rhs_scale=plane_0[:, lo:hi],
+                start=True,
+                stop=True,
+            )
+        open_groups(0)
+        quantize_w(0, 2, 4)
+        open_groups(1)
         for a in range(2):
-            gather(scalar_copy, late[a][:, 0, :], 1, 2, a * HALF, (a + 1) * HALF)
-            gather(vector_copy, late[a][:, 1, :], 1, 3, a * HALF, (a + 1) * HALF)
-        weave_pair(vector_copy, 0, 1, late[0][:])
-        weave_pair(vector_copy, 1, 1, late[1][:], 0, 64)
-        weave_pair(scalar_copy, 1, 1, late[1][:], 64, HALF)
+            gather_half(3, a)
+            weave_pair(1, a)
         quantize_x(0, "x_plane_1_0")
         cast_w(scalar_copy, 1, 0, 86, P)
         cast_w(vector_copy, 1, 0, 0, 86)
@@ -185,6 +210,9 @@ def tile_picked_dconv_none_e_kernel(tc, xT, w1, w2_words, w2_scales, taps, offs,
         z_codes = keep.tile([P, S], U32, name="z_codes", align_bytes=64)
         z_plane = keep.tile([P, S], U8, name="z_plane", align_bytes=64)
         for t, lo, hi, bank in groups:
+            if (t, lo) not in banks:
+                banks[t, lo] = psum.tile([P, hi - lo], F32, name="h_%d_%d" % (t, lo), tag=bank)
+                first_product(banks[t, lo], 0, t, lo, hi, True)
             h = banks[t, lo]
             first_product(h, 1, t, lo, hi, False)
             nc.scalar.activation(out=delayed[:, t, lo + 1 : hi + 1], in_=h[:], func=COPY, scale=tap[:, t, 1:2])
@@ -243,6 +271,5 @@ def tile_picked_dconv_none_e_kernel(tc, xT, w1, w2_words, w2_scales, taps, offs,
         quantize_z(3)
         quantize_z(2)
         second_product(vector_copy, 3 * QUARTER, S, "bank_0_1")
-        nc.sync.dma_start(out=out[:, 3 * QUARTER : S], in_=result[1][:, QUARTER:HALF])
         second_product(vector_copy, HALF, 3 * QUARTER, "bank_0_2")
-        nc.sync.dma_start(out=out[:, HALF : 3 * QUARTER], in_=result[1][:, 0:QUARTER])
+        nc.sync.dma_start(out=out[:, HALF:S], in_=result[1][:])

@@ -76,7 +76,8 @@ def tile_picked_dconv_none_e_kernel(tc, xT, w1, w2_words, w2_scales, taps, offs,
         nc.sync.dma_start(out=tap[:], in_=taps.rearrange("(p t) d -> p t d", t=PACK))
         nc.sync.dma_start(out=w2_codes[:].bitcast(I32), in_=w2_words[0].bitcast(I32))
         for q in range(4):
-            nc.sync.dma_start(
+            queue = nc.gpsimd if q == 0 else nc.sync
+            queue.dma_start(
                 out=w2_plane[32 * q : 32 * q + 4, :].bitcast(I32), in_=w2_scales[0, 4 * q : 4 * q + 4, :].bitcast(I32)
             )
 
@@ -271,5 +272,6 @@ def tile_picked_dconv_none_e_kernel(tc, xT, w1, w2_words, w2_scales, taps, offs,
         quantize_z(3)
         quantize_z(2)
         second_product(vector_copy, 3 * QUARTER, S, "bank_0_1")
+        nc.sync.dma_start(out=out[:, 3 * QUARTER : S], in_=result[1][:, QUARTER:HALF])
         second_product(vector_copy, HALF, 3 * QUARTER, "bank_0_2")
-        nc.sync.dma_start(out=out[:, HALF:S], in_=result[1][:])
+        nc.sync.dma_start(out=out[:, HALF : 3 * QUARTER], in_=result[1][:, 0:QUARTER])

@@ -68,16 +68,14 @@ def tile_picked_dconv_none_e_kernel(tc, xT, w1, w2_words, w2_scales, taps, offs,
         load_x(0, 0, 2)
         nc.sync.dma_start(offsets[:], offs)
         load_x(0, 2, 4)
-        load_x(1, 0, 2)
-        load_x(1, 2, 3)
+        load_x(1, 0, 3)
         load_w(0)
         load_x(1, 3, 4)
         load_w(1)
         nc.sync.dma_start(out=tap[:], in_=taps.rearrange("(p t) d -> p t d", t=PACK))
         nc.sync.dma_start(out=w2_codes[:].bitcast(I32), in_=w2_words[0].bitcast(I32))
         for q in range(4):
-            queue = nc.gpsimd if q == 0 else nc.sync
-            queue.dma_start(
+            nc.sync.dma_start(
                 out=w2_plane[32 * q : 32 * q + 4, :].bitcast(I32), in_=w2_scales[0, 4 * q : 4 * q + 4, :].bitcast(I32)
             )
 
@@ -103,15 +101,15 @@ def tile_picked_dconv_none_e_kernel(tc, xT, w1, w2_words, w2_scales, taps, offs,
         for u in range(2):
             for a in range(2):
                 picked_1[u, a] = keep.tile([P, 2, HALF], F32, name="picked_1_%d_%d" % (u, a))
-        quads_1 = [keep.tile([P, HALF * PACK], BF16, name="quads_1_%d" % a, align_bytes=64) for a in range(2)]
+        quads_1 = {0: keep.tile([P, HALF * PACK], BF16, name="quads_1_0", align_bytes=64)}
 
-        def gather_half(j, a):
-            gather(scalar_copy, picked_1[j // 2, a][:, j % 2, :], 1, j, a * HALF, (a + 1) * HALF)
+        def gather_half(copy, j, a):
+            gather(copy, picked_1[j // 2, a][:, j % 2, :], 1, j, a * HALF, (a + 1) * HALF)
 
-        def weave_pair(u, a):
-            vector_copy(
-                quads_1[a][:].rearrange("p (c i j) -> p c j i", i=4, j=PACK)[:, :, 2 * u : 2 * u + 2, :],
-                picked_1[u, a][:].rearrange("p j (c i) -> p c j i", i=4),
+        def weave_pair(u, a, copy=vector_copy, lo=0, hi=HALF):
+            copy(
+                quads_1[a][:].rearrange("p (c i j) -> p c j i", i=4, j=PACK)[:, lo // 4 : hi // 4, 2 * u : 2 * u + 2, :],
+                picked_1[u, a][:].rearrange("p j (c i) -> p c j i", i=4)[:, lo // 4 : hi // 4, :, :],
             )
 
         def quantize_x(a, tag):
@@ -123,12 +121,12 @@ def tile_picked_dconv_none_e_kernel(tc, xT, w1, w2_words, w2_scales, taps, offs,
         for a in range(2):
             x_plane[0, a] = plane_0[:, halves[a]]
         nc.vector.quantize_mx(out=x_codes[0][:].bitcast(FP8X4), scales=plane_0[:], in_=quads_0[:])
+        for a, copy in ((0, scalar_copy), (1, vector_copy)):
+            gather_half(copy, 0, a)
+            gather_half(copy, 1, a)
+        weave_pair(0, 0)
         for a in range(2):
-            gather_half(0, a)
-            gather_half(1, a)
-            weave_pair(0, a)
-        for a in range(2):
-            gather_half(2, a)
+            gather_half(scalar_copy, 2, a)
 
         w_codes = [keep.tile([P, H], U32, name="w_codes_%d" % c, align_bytes=64) for c in range(PASSES)]
         w_bf, w_plane = {}, {}
@@ -152,8 +150,9 @@ def tile_picked_dconv_none_e_kernel(tc, xT, w1, w2_words, w2_scales, taps, offs,
                 in_=w_bf[c, t0 // 2][:, t0 % 2 : t0 % 2 + t1 - t0, :, :].rearrange("p t m j -> p (t m j)"),
             )
 
-        groups = [(t, a * HALF, (a + 1) * HALF, "bank_%d_%d" % (a, t)) for a in range(2) for t in range(PACK)][:-1]
-        groups = groups + [(3, HALF, 3 * QUARTER, "bank_1_3"), (3, 3 * QUARTER, S, "bank_0_0")]
+        groups = [(t, a * HALF, (a + 1) * HALF, "bank_%d" % (PACK * a + t)) for a in range(2) for t in range(PACK)]
+        groups = [(0, 0, QUARTER, "bank_0"), (0, QUARTER, HALF, "bank_7")] + groups[1:-1]
+        groups = groups + [(3, HALF, 3 * QUARTER, "bank_0"), (3, 3 * QUARTER, S, "bank_7")]
 
         def first_product(acc, c, t, lo, hi, first):
             cols = slice(t * P, (t + 1) * P)
@@ -170,17 +169,17 @@ def tile_picked_dconv_none_e_kernel(tc, xT, w1, w2_words, w2_scales, taps, offs,
         banks = {}
 
         def open_groups(g):
-            for t, lo, hi, bank in groups[:-1]:
+            for t, lo, hi, bank in groups[:-2]:
                 if t // 2 == g:
                     banks[t, lo] = psum.tile([P, hi - lo], F32, name="h_%d_%d" % (t, lo), tag=bank)
                     first_product(banks[t, lo], 0, t, lo, hi, True)
 
         cast_w(vector_copy, 0, 0, 0, P)
-        cast_w(scalar_copy, 0, 1, 92, P)
-        cast_w(vector_copy, 0, 1, 0, 92)
+        cast_w(scalar_copy, 0, 1, 52, P)
+        cast_w(vector_copy, 0, 1, 0, 52)
         quantize_w(0, 0, 1)
         quantize_w(0, 1, 2)
-        warm = psum.tile([P, S], F32, name="warm", tag="bank_1_3")
+        warm = psum.tile([P, S], F32, name="warm", tag="bank_7")
         for lo, hi in ((0, HALF), (HALF, 3 * QUARTER)):
             nc.tensor.matmul_mx(
                 out=warm[:, lo:hi],
@@ -194,9 +193,13 @@ def tile_picked_dconv_none_e_kernel(tc, xT, w1, w2_words, w2_scales, taps, offs,
         open_groups(0)
         quantize_w(0, 2, 4)
         open_groups(1)
-        for a in range(2):
-            gather_half(3, a)
-            weave_pair(1, a)
+        quads_1[1] = keep.tile([P, HALF * PACK], BF16, name="quads_1_1", tag="w_bf_0_0", align_bytes=64)
+        weave_pair(0, 1)
+        gather_half(scalar_copy, 3, 0)
+        weave_pair(1, 0)
+        gather_half(scalar_copy, 3, 1)
+        weave_pair(1, 1, scalar_copy, QUARTER, HALF)
+        weave_pair(1, 1, vector_copy, 0, QUARTER)
         quantize_x(0, "x_plane_1_0")
         cast_w(scalar_copy, 1, 0, 86, P)
         cast_w(vector_copy, 1, 0, 0, 86)
@@ -267,11 +270,11 @@ def tile_picked_dconv_none_e_kernel(tc, xT, w1, w2_words, w2_scales, taps, offs,
         weave_z(vector_copy, 3)
         weave_z(scalar_copy, 2)
         quantize_z(1)
-        second_product(scalar_copy, 0, HALF, "bank_0_3")
+        second_product(scalar_copy, 0, HALF, "bank_3")
         nc.sync.dma_start(out=out[:, 0:HALF], in_=result[0][:])
         quantize_z(3)
         quantize_z(2)
-        second_product(vector_copy, 3 * QUARTER, S, "bank_0_1")
+        second_product(vector_copy, 3 * QUARTER, S, "bank_1")
         nc.sync.dma_start(out=out[:, 3 * QUARTER : S], in_=result[1][:, QUARTER:HALF])
-        second_product(vector_copy, HALF, 3 * QUARTER, "bank_0_2")
+        second_product(vector_copy, HALF, 3 * QUARTER, "bank_2")
         nc.sync.dma_start(out=out[:, HALF : 3 * QUARTER], in_=result[1][:, 0:QUARTER])

@@ -97,20 +97,11 @@ def tile_picked_dconv_none_e_kernel(tc, xT, w1, w2_words, w2_scales, taps, offs,
             gather(vector_copy if j % 2 else scalar_copy, picked_0[:, j, :], 0, j, 0, S)
         quads_0 = keep.tile([P, S * PACK], BF16, name="quads_0", align_bytes=64)
         weave(vector_copy, quads_0, picked_0, 0, PACK, 0, S)
-        picked_1 = {}
-        for u in range(2):
-            for a in range(2):
-                picked_1[u, a] = keep.tile([P, 2, HALF], F32, name="picked_1_%d_%d" % (u, a))
+        picked_1 = [keep.tile([P, PACK, HALF], F32, name="picked_1_%d" % a) for a in range(2)]
         quads_1 = {0: keep.tile([P, HALF * PACK], BF16, name="quads_1_0", align_bytes=64)}
 
         def gather_half(copy, j, a):
-            gather(copy, picked_1[j // 2, a][:, j % 2, :], 1, j, a * HALF, (a + 1) * HALF)
-
-        def weave_pair(u, a, copy=vector_copy, lo=0, hi=HALF):
-            copy(
-                quads_1[a][:].rearrange("p (c i j) -> p c j i", i=4, j=PACK)[:, lo // 4 : hi // 4, 2 * u : 2 * u + 2, :],
-                picked_1[u, a][:].rearrange("p j (c i) -> p c j i", i=4)[:, lo // 4 : hi // 4, :, :],
-            )
+            gather(copy, picked_1[a][:, j, :], 1, j, a * HALF, (a + 1) * HALF)
 
         def quantize_x(a, tag):
             plane = keep.tile([P, HALF], U8, name="x_plane_1_%d" % a, tag=tag, align_bytes=64)
@@ -124,7 +115,7 @@ def tile_picked_dconv_none_e_kernel(tc, xT, w1, w2_words, w2_scales, taps, offs,
         for a, copy in ((0, scalar_copy), (1, vector_copy)):
             gather_half(copy, 0, a)
             gather_half(copy, 1, a)
-        weave_pair(0, 0)
+        weave(vector_copy, quads_1[0], picked_1[0], 0, 2, 0, HALF)
         for a in range(2):
             gather_half(scalar_copy, 2, a)
 
@@ -194,12 +185,12 @@ def tile_picked_dconv_none_e_kernel(tc, xT, w1, w2_words, w2_scales, taps, offs,
         quantize_w(0, 2, 4)
         open_groups(1)
         quads_1[1] = keep.tile([P, HALF * PACK], BF16, name="quads_1_1", tag="w_bf_0_0", align_bytes=64)
-        weave_pair(0, 1)
+        weave(vector_copy, quads_1[1], picked_1[1], 0, 2, 0, QUARTER)
         gather_half(scalar_copy, 3, 0)
-        weave_pair(1, 0)
+        weave(vector_copy, quads_1[0], picked_1[0], 2, PACK, 0, HALF)
         gather_half(scalar_copy, 3, 1)
-        weave_pair(1, 1, scalar_copy, QUARTER, HALF)
-        weave_pair(1, 1, vector_copy, 0, QUARTER)
+        weave(scalar_copy, quads_1[1], picked_1[1], 0, PACK, QUARTER, HALF)
+        weave(vector_copy, quads_1[1], picked_1[1], 2, PACK, 0, QUARTER)
         quantize_x(0, "x_plane_1_0")
         cast_w(scalar_copy, 1, 0, 86, P)
         cast_w(vector_copy, 1, 0, 0, 86)

@@ -170,17 +170,6 @@ def tile_picked_dconv_none_e_kernel(tc, xT, w1, w2_words, w2_scales, taps, offs,
         cast_w(vector_copy, 0, 1, 0, 52)
         quantize_w(0, 0, 1)
         quantize_w(0, 1, 2)
-        warm = psum.tile([P, S], F32, name="warm", tag="bank_7")
-        for lo, hi in ((0, HALF), (HALF, 3 * QUARTER)):
-            nc.tensor.matmul_mx(
-                out=warm[:, lo:hi],
-                lhsT=w_codes[0][:, 0:P].bitcast(FP8X4),
-                lhsT_scale=w_plane[0, 0][:, 0:P],
-                rhs=x_codes[0][:, lo:hi].bitcast(FP8X4),
-                rhs_scale=plane_0[:, lo:hi],
-                start=True,
-                stop=True,
-            )
         open_groups(0)
         quantize_w(0, 2, 4)
         open_groups(1)

@@ -143,7 +143,7 @@ def tile_picked_dconv_none_e_kernel(tc, xT, w1, w2_words, w2_scales, taps, offs,
 
         groups = [(t, a * HALF, (a + 1) * HALF, "bank_%d" % (PACK * a + t)) for a in range(2) for t in range(PACK)]
         groups = [(0, 0, QUARTER, "bank_0"), (0, QUARTER, HALF, "bank_7")] + groups[1:-1]
-        groups = groups + [(3, HALF, 3 * QUARTER, "bank_0"), (3, 3 * QUARTER, S, "bank_7")]
+        groups = groups + [(3, HALF, 3 * QUARTER, "bank_7"), (3, 3 * QUARTER, S, "bank_1")]
 
         def first_product(acc, c, t, lo, hi, first):
             cols = slice(t * P, (t + 1) * P)
@@ -166,8 +166,8 @@ def tile_picked_dconv_none_e_kernel(tc, xT, w1, w2_words, w2_scales, taps, offs,
                     first_product(banks[t, lo], 0, t, lo, hi, True)
 
         cast_w(vector_copy, 0, 0, 0, P)
-        cast_w(scalar_copy, 0, 1, 52, P)
-        cast_w(vector_copy, 0, 1, 0, 52)
+        cast_w(scalar_copy, 0, 1, 76, P)
+        cast_w(vector_copy, 0, 1, 0, 76)
         quantize_w(0, 0, 1)
         quantize_w(0, 1, 2)
         open_groups(0)
@@ -190,7 +190,6 @@ def tile_picked_dconv_none_e_kernel(tc, xT, w1, w2_words, w2_scales, taps, offs,
         quantize_x(1, "w_bf_1_0")
 
         z_rows = [keep.tile([P, PACK, HALF], F32, name="z_rows_%d" % a) for a in range(2)]
-        z_bf = keep.tile([P, S * PACK], BF16, name="z_bf", align_bytes=64)
         z_codes = keep.tile([P, S], U32, name="z_codes", align_bytes=64)
         z_plane = keep.tile([P, S], U8, name="z_plane", align_bytes=64)
         for t, lo, hi, bank in groups:
@@ -209,10 +208,14 @@ def tile_picked_dconv_none_e_kernel(tc, xT, w1, w2_words, w2_scales, taps, offs,
                 op1=ADD,
             )
 
+        z_bf = {}
+        for q in range(4):
+            z_bf[q] = keep.tile([P, QUARTER * PACK], BF16, name="z_bf_%d" % q, align_bytes=64)
+
         def weave_z(copy, q):
             a, lo = q // 2, (q % 2) * QUARTER
             copy(
-                z_bf[:, q * QUARTER * PACK : (q + 1) * QUARTER * PACK].rearrange("p (c i t) -> p c t i", i=4, t=PACK),
+                z_bf[q][:].rearrange("p (c i t) -> p c t i", i=4, t=PACK),
                 z_rows[a][:, :, lo : lo + QUARTER].rearrange("p t (c i) -> p c t i", i=4),
             )
 
@@ -221,7 +224,7 @@ def tile_picked_dconv_none_e_kernel(tc, xT, w1, w2_words, w2_scales, taps, offs,
         def quantize_z(q):
             lo, hi = q * QUARTER, (q + 1) * QUARTER
             nc.vector.quantize_mx(
-                out=z_codes[:, lo:hi].bitcast(FP8X4), scales=z_plane[:, lo:hi], in_=z_bf[:, lo * PACK : hi * PACK]
+                out=z_codes[:, lo:hi].bitcast(FP8X4), scales=z_plane[:, lo:hi], in_=z_bf[q][:]
             )
 
         def second_product(copy, lo, hi, bank):
@@ -238,7 +241,7 @@ def tile_picked_dconv_none_e_kernel(tc, xT, w1, w2_words, w2_scales, taps, offs,
             copy(result[lo // HALF][:, lo % HALF : lo % HALF + hi - lo], acc[:])
 
         nc.gpsimd.tensor_scalar(
-            z_bf[:, 0 : QUARTER * PACK].rearrange("p (n t) -> p n t", t=PACK),
+            z_bf[0][:].rearrange("p (n t) -> p n t", t=PACK),
             z_rows[0][:, :, 0:QUARTER].rearrange("p t n -> p n t"),
             1.0,
             0.0,
@@ -250,11 +253,11 @@ def tile_picked_dconv_none_e_kernel(tc, xT, w1, w2_words, w2_scales, taps, offs,
         weave_z(vector_copy, 3)
         weave_z(scalar_copy, 2)
         quantize_z(1)
-        second_product(scalar_copy, 0, HALF, "bank_3")
+        second_product(scalar_copy, 0, HALF, "bank_0")
         nc.sync.dma_start(out=out[:, 0:HALF], in_=result[0][:])
         quantize_z(3)
         quantize_z(2)
-        second_product(vector_copy, 3 * QUARTER, S, "bank_1")
+        second_product(vector_copy, 3 * QUARTER, S, "bank_3")
         nc.sync.dma_start(out=out[:, 3 * QUARTER : S], in_=result[1][:, QUARTER:HALF])
         second_product(vector_copy, HALF, 3 * QUARTER, "bank_2")
         nc.sync.dma_start(out=out[:, HALF : 3 * QUARTER], in_=result[1][:, 0:QUARTER])

@@ -31,6 +31,9 @@ def tile_picked_dconv_none_e_kernel(tc, xT, w1, w2_words, w2_scales, taps, offs,
     def scalar_copy(dst, src):
         nc.scalar.activation(out=dst, in_=src, func=COPY)
 
+    def scalar_move(dst, src):
+        nc.scalar.copy(out=dst, in_=src)
+
     def vector_copy(dst, src):
         nc.vector.tensor_copy(out=dst, in_=src)
 
@@ -189,7 +192,7 @@ def tile_picked_dconv_none_e_kernel(tc, xT, w1, w2_words, w2_scales, taps, offs,
             quantize_w(1, t, t + 1)
         quantize_x(1, "w_bf_1_0")
 
-        z_rows = [keep.tile([P, PACK, HALF], F32, name="z_rows_%d" % a) for a in range(2)]
+        z_rows = [keep.tile([P, PACK, HALF], BF16, name="z_rows_%d" % a) for a in range(2)]
         z_codes = keep.tile([P, S], U32, name="z_codes", align_bytes=64)
         z_plane = keep.tile([P, S], U8, name="z_plane", align_bytes=64)
         for t, lo, hi, bank in groups:
@@ -248,10 +251,10 @@ def tile_picked_dconv_none_e_kernel(tc, xT, w1, w2_words, w2_scales, taps, offs,
             MULT,
             ADD,
         )
-        weave_z(scalar_copy, 1)
+        weave_z(scalar_move, 1)
         quantize_z(0)
         weave_z(vector_copy, 3)
-        weave_z(scalar_copy, 2)
+        weave_z(scalar_move, 2)
         quantize_z(1)
         second_product(scalar_copy, 0, HALF, "bank_0")
         nc.sync.dma_start(out=out[:, 0:HALF], in_=result[0][:])

@@ -57,13 +57,13 @@ def tile_picked_dconv_none_e_kernel(tc, xT, w1, w2_words, w2_scales, taps, offs,
 
         def load_x(c, j0, j1):
             rows = xT[c * K_PASS : (c + 1) * K_PASS, :].rearrange("(p j) n -> p (j n)", j=PACK)
-            raw = keep.tile([P, (j1 - j0) * T], F32, name="x_raw_%d_%d" % (c, j0), align_bytes=64)
+            raw = keep.tile([P, (j1 - j0) * T], F32, name="x_raw_%d_%d" % (c, j0), align_bytes=256)
             nc.sync.dma_start(out=raw[:], in_=rows[:, j0 * T : j1 * T])
             for j in range(j0, j1):
                 x_raw[c, j] = raw[:, (j - j0) * T : (j - j0 + 1) * T]
 
         def load_w(c):
-            w_raw[c] = keep.tile([P, PACK, H], F32, name="w_raw_%d" % c, align_bytes=64)
+            w_raw[c] = keep.tile([P, PACK, H], F32, name="w_raw_%d" % c, align_bytes=256)
             nc.sync.dma_start(
                 out=w_raw[c][:], in_=w1[c * K_PASS : (c + 1) * K_PASS, :].rearrange("(p j) n -> p j n", j=PACK)
             )
@@ -222,7 +222,7 @@ def tile_picked_dconv_none_e_kernel(tc, xT, w1, w2_words, w2_scales, taps, offs,
                 z_rows[a][:, :, lo : lo + QUARTER].rearrange("p t (c i) -> p c t i", i=4),
             )
 
-        result = [keep.tile([P, HALF], F32, name="result_%d" % a) for a in range(2)]
+        result = [keep.tile([P, HALF], F32, name="result_%d" % a, align_bytes=256) for a in range(2)]
 
         def quantize_z(q):
             lo, hi = q * QUARTER, (q + 1) * QUARTER

@@ -57,13 +57,13 @@ def tile_picked_dconv_none_e_kernel(tc, xT, w1, w2_words, w2_scales, taps, offs,
 
         def load_x(c, j0, j1):
             rows = xT[c * K_PASS : (c + 1) * K_PASS, :].rearrange("(p j) n -> p (j n)", j=PACK)
-            raw = keep.tile([P, (j1 - j0) * T], F32, name="x_raw_%d_%d" % (c, j0), align_bytes=256)
+            raw = keep.tile([P, (j1 - j0) * T], F32, name="x_raw_%d_%d" % (c, j0), align_bytes=1024)
             nc.sync.dma_start(out=raw[:], in_=rows[:, j0 * T : j1 * T])
             for j in range(j0, j1):
                 x_raw[c, j] = raw[:, (j - j0) * T : (j - j0 + 1) * T]
 
         def load_w(c):
-            w_raw[c] = keep.tile([P, PACK, H], F32, name="w_raw_%d" % c, align_bytes=256)
+            w_raw[c] = keep.tile([P, PACK, H], F32, name="w_raw_%d" % c, align_bytes=1024)
             nc.sync.dma_start(
                 out=w_raw[c][:], in_=w1[c * K_PASS : (c + 1) * K_PASS, :].rearrange("(p j) n -> p j n", j=PACK)
             )
@@ -222,7 +222,7 @@ def tile_picked_dconv_none_e_kernel(tc, xT, w1, w2_words, w2_scales, taps, offs,
                 z_rows[a][:, :, lo : lo + QUARTER].rearrange("p t (c i) -> p c t i", i=4),
             )
 
-        result = [keep.tile([P, HALF], F32, name="result_%d" % a, align_bytes=256) for a in range(2)]
+        result = [keep.tile([P, HALF], F32, name="result_%d" % a, align_bytes=1024) for a in range(2)]
 
         def quantize_z(q):
             lo, hi = q * QUARTER, (q + 1) * QUARTER

@@ -39,7 +39,6 @@ def tile_picked_dconv_none_e_kernel(tc, xT, w1, w2_words, w2_scales, taps, offs,
 
     with ExitStack() as ctx:
         keep = ctx.enter_context(tc.tile_pool(name="keep", bufs=1))
-        stage = ctx.enter_context(tc.tile_pool(name="stage", bufs=1))
         psum = ctx.enter_context(tc.psum_pool(name="psum", bufs=1))
 
         offsets = keep.tile([P, S // 16], U16, name="offsets")
@@ -215,11 +214,11 @@ def tile_picked_dconv_none_e_kernel(tc, xT, w1, w2_words, w2_scales, taps, offs,
         for q in range(4):
             z_bf[q] = keep.tile([P, QUARTER * PACK], BF16, name="z_bf_%d" % q, align_bytes=64)
 
-        def weave_z(copy, q):
+        def weave_z(copy, q, n0=0, n1=QUARTER):
             a, lo = q // 2, (q % 2) * QUARTER
             copy(
-                z_bf[q][:].rearrange("p (c i t) -> p c t i", i=4, t=PACK),
-                z_rows[a][:, :, lo : lo + QUARTER].rearrange("p t (c i) -> p c t i", i=4),
+                z_bf[q][:].rearrange("p (c i t) -> p c t i", i=4, t=PACK)[:, n0 // 4 : n1 // 4, :, :],
+                z_rows[a][:, :, lo + n0 : lo + n1].rearrange("p t (c i) -> p c t i", i=4),
             )
 
         result = [keep.tile([P, HALF], F32, name="result_%d" % a, align_bytes=1024) for a in range(2)]
@@ -253,10 +252,12 @@ def tile_picked_dconv_none_e_kernel(tc, xT, w1, w2_words, w2_scales, taps, offs,
         )
         weave_z(scalar_move, 1)
         quantize_z(0)
+        weave_z(vector_copy, 2, 0, 40)
         weave_z(vector_copy, 3)
-        weave_z(scalar_move, 2)
+        weave_z(scalar_move, 2, 40, QUARTER)
+        second_product(scalar_move, 0, QUARTER, "bank_0")
         quantize_z(1)
-        second_product(scalar_copy, 0, HALF, "bank_0")
+        second_product(scalar_move, QUARTER, HALF, "bank_4")
         nc.sync.dma_start(out=out[:, 0:HALF], in_=result[0][:])
         quantize_z(3)
         quantize_z(2)

@@ -243,8 +243,8 @@ def tile_picked_dconv_none_e_kernel(tc, xT, w1, w2_words, w2_scales, taps, offs,
             copy(result[lo // HALF][:, lo % HALF : lo % HALF + hi - lo], acc[:])
 
         nc.gpsimd.tensor_scalar(
-            z_bf[0][:].rearrange("p (n t) -> p n t", t=PACK),
-            z_rows[0][:, :, 0:QUARTER].rearrange("p t n -> p n t"),
+            z_bf[0][:].rearrange("p (c i t) -> p c t i", i=4, t=PACK),
+            z_rows[0][:, :, 0:QUARTER].rearrange("p t (c i) -> p c t i", i=4),
             1.0,
             0.0,
             MULT,

from contextlib import ExitStack

import concourse.mybir as mybir

K, T, S, H, N = 1024, 1024, 512, 512, 128
FLOPS = 2 * K * H * S + 2 * H * N * S

F32 = mybir.dt.float32
BF16 = mybir.dt.bfloat16
I32 = mybir.dt.int32
U32 = mybir.dt.uint32
U16 = mybir.dt.uint16
U8 = mybir.dt.uint8
FP8X4 = mybir.dt.float8_e4m3fn_x4
FP4X4 = mybir.dt.float4_e2m1fn_x4
COPY = mybir.ActivationFunctionType.Copy
MULT = mybir.AluOpType.mult
ADD = mybir.AluOpType.add

P = 128
PACK = 4
K_PASS = P * PACK
PASSES = K // K_PASS
HALF = S // 2
QUARTER = S // 4


def tile_picked_dconv_none_e_kernel(tc, xT, w1, w2_words, w2_scales, taps, offs, out):
    nc = tc.nc

    def scalar_copy(dst, src):
        nc.scalar.activation(out=dst, in_=src, func=COPY)

    def scalar_move(dst, src):
        nc.scalar.copy(out=dst, in_=src)

    def vector_copy(dst, src):
        nc.vector.tensor_copy(out=dst, in_=src)

    with ExitStack() as ctx:
        keep = ctx.enter_context(tc.tile_pool(name="keep", bufs=1))
        psum = ctx.enter_context(tc.psum_pool(name="psum", bufs=1))

        offsets = keep.tile([P, S // 16], U16, name="offsets")
        w2_codes = keep.tile([P, 2 * N], U8, name="w2_codes", align_bytes=64)
        w2_plane = keep.tile([P, N], U8, name="w2_plane", align_bytes=64)
        tap = keep.tile([P, PACK, 2], F32, name="tap")
        delayed = keep.tile([P, PACK, S + 8], F32, name="delayed")

        nc.vector.memset(w2_plane[:].bitcast(I32), 0)
        zero = keep.tile([P, PACK, 1], F32, name="zero")
        nc.vector.memset(zero[:], 0.0)
        scalar_copy(delayed[:, :, 0:1], zero[:])

        x_raw, w_raw = {}, {}

        def load_x(c, j0, j1):
            rows = xT[c * K_PASS : (c + 1) * K_PASS, :].rearrange("(p j) n -> p (j n)", j=PACK)
            raw = keep.tile([P, (j1 - j0) * T], F32, name="x_raw_%d_%d" % (c, j0), align_bytes=1024)
            nc.sync.dma_start(out=raw[:], in_=rows[:, j0 * T : j1 * T])
            for j in range(j0, j1):
                x_raw[c, j] = raw[:, (j - j0) * T : (j - j0 + 1) * T]

        def load_w(c):
            w_raw[c] = keep.tile([P, PACK, H], F32, name="w_raw_%d" % c, align_bytes=1024)
            nc.sync.dma_start(
                out=w_raw[c][:], in_=w1[c * K_PASS : (c + 1) * K_PASS, :].rearrange("(p j) n -> p j n", j=PACK)
            )

        load_x(0, 0, 2)
        nc.sync.dma_start(offsets[:], offs)
        load_x(0, 2, 4)
        load_x(1, 0, 3)
        load_w(0)
        load_x(1, 3, 4)
        load_w(1)
        nc.sync.dma_start(out=tap[:], in_=taps.rearrange("(p t) d -> p t d", t=PACK))
        nc.sync.dma_start(out=w2_codes[:].bitcast(I32), in_=w2_words[0].bitcast(I32))
        for q in range(4):
            nc.sync.dma_start(
                out=w2_plane[32 * q : 32 * q + 4, :].bitcast(I32), in_=w2_scales[0, 4 * q : 4 * q + 4, :].bitcast(I32)
            )

        halves = [slice(a * HALF, (a + 1) * HALF) for a in range(2)]
        x_codes = [keep.tile([P, S], U32, name="x_codes_%d" % c, align_bytes=64) for c in range(PASSES)]
        x_plane = {}

        def gather(copy, dst, c, j, lo, hi):
            copy(dst, x_raw[c, j].indirect(offsets[:, lo // 16 : hi // 16]))

        def weave(copy, quads, picked, j0, j1, lo, hi):
            copy(
                quads[:].rearrange("p (c i j) -> p c j i", i=4, j=PACK)[:, lo // 4 : hi // 4, j0:j1, :],
                picked[:].rearrange("p j (c i) -> p c j i", i=4)[:, lo // 4 : hi // 4, j0:j1, :],
            )

        picked_0 = keep.tile([P, PACK, S], F32, name="picked_0")
        for j in range(PACK):
            gather(vector_copy if j % 2 else scalar_copy, picked_0[:, j, :], 0, j, 0, S)
        quads_0 = keep.tile([P, S * PACK], BF16, name="quads_0", align_bytes=64)
        weave(vector_copy, quads_0, picked_0, 0, PACK, 0, S)
        picked_1 = [keep.tile([P, PACK, HALF], F32, name="picked_1_%d" % a) for a in range(2)]
        quads_1 = {0: keep.tile([P, HALF * PACK], BF16, name="quads_1_0", align_bytes=64)}

        def gather_half(copy, j, a):
            gather(copy, picked_1[a][:, j, :], 1, j, a * HALF, (a + 1) * HALF)

        def quantize_x(a, tag):
            plane = keep.tile([P, HALF], U8, name="x_plane_1_%d" % a, tag=tag, align_bytes=64)
            x_plane[1, a] = plane[:]
            nc.vector.quantize_mx(out=x_codes[1][:, halves[a]].bitcast(FP8X4), scales=plane[:], in_=quads_1[a][:])

        plane_0 = keep.tile([P, S], U8, name="x_plane_0", align_bytes=64)
        for a in range(2):
            x_plane[0, a] = plane_0[:, halves[a]]
        nc.vector.quantize_mx(out=x_codes[0][:].bitcast(FP8X4), scales=plane_0[:], in_=quads_0[:])
        for a, copy in ((0, scalar_copy), (1, vector_copy)):
            gather_half(copy, 0, a)
            gather_half(copy, 1, a)
        weave(vector_copy, quads_1[0], picked_1[0], 0, 2, 0, HALF)
        for a in range(2):
            gather_half(scalar_copy, 2, a)

        w_codes = [keep.tile([P, H], U32, name="w_codes_%d" % c, align_bytes=64) for c in range(PASSES)]
        w_bf, w_plane = {}, {}
        for c in range(PASSES):
            for g in range(2):
                w_bf[c, g] = keep.tile([P, 2, P, PACK], BF16, name="w_bf_%d_%d" % (c, g), align_bytes=64)
                plane = keep.tile([P, H // 2], U8, name="w_plane_%d_%d" % (c, g), align_bytes=64)
                w_plane[c, g] = plane[:]

        def cast_w(copy, c, g, m0, m1):
            copy(
                w_bf[c, g][:].rearrange("p t m j -> p m j t")[:, m0:m1, :, :],
                w_raw[c][:].rearrange("p j (m t) -> p m j t", t=PACK)[:, m0:m1, :, 2 * g : 2 * g + 2],
            )

        def quantize_w(c, t0, t1):
            cols = slice(t0 * P, t1 * P)
            nc.vector.quantize_mx(
                out=w_codes[c][:, cols].bitcast(FP8X4),
                scales=w_plane[c, t0 // 2][:, (t0 % 2) * P : (t0 % 2 + t1 - t0) * P],
                in_=w_bf[c, t0 // 2][:, t0 % 2 : t0 % 2 + t1 - t0, :, :].rearrange("p t m j -> p (t m j)"),
            )

        groups = [(t, a * HALF, (a + 1) * HALF, "bank_%d" % (PACK * a + t)) for a in range(2) for t in range(PACK)]
        groups = [(0, 0, QUARTER, "bank_0"), (0, QUARTER, HALF, "bank_7")] + groups[1:-1]
        groups = groups + [(3, HALF, 3 * QUARTER, "bank_7"), (3, 3 * QUARTER, S, "bank_1")]

        def first_product(acc, c, t, lo, hi, first):
            cols = slice(t * P, (t + 1) * P)
            nc.tensor.matmul_mx(
                out=acc[:],
                lhsT=w_codes[c][:, cols].bitcast(FP8X4),
                lhsT_scale=w_plane[c, t // 2][:, (t % 2) * P : (t % 2 + 1) * P],
                rhs=x_codes[c][:, lo:hi].bitcast(FP8X4),
                rhs_scale=x_plane[c, lo // HALF][:, lo % HALF : lo % HALF + hi - lo],
                start=first,
                stop=not first,
            )

        banks = {}

        def open_groups(g):
            for t, lo, hi, bank in groups[:-2]:
                if t // 2 == g:
                    banks[t, lo] = psum.tile([P, hi - lo], F32, name="h_%d_%d" % (t, lo), tag=bank)
                    first_product(banks[t, lo], 0, t, lo, hi, True)

        cast_w(vector_copy, 0, 0, 0, P)
        cast_w(scalar_copy, 0, 1, 76, P)
        cast_w(vector_copy, 0, 1, 0, 76)
        quantize_w(0, 0, 1)
        quantize_w(0, 1, 2)
        open_groups(0)
        quantize_w(0, 2, 4)
        open_groups(1)
        quads_1[1] = keep.tile([P, HALF * PACK], BF16, name="quads_1_1", tag="w_bf_0_0", align_bytes=64)
        weave(vector_copy, quads_1[1], picked_1[1], 0, 2, 0, QUARTER)
        gather_half(scalar_copy, 3, 0)
        weave(vector_copy, quads_1[0], picked_1[0], 2, PACK, 0, HALF)
        gather_half(scalar_copy, 3, 1)
        weave(scalar_copy, quads_1[1], picked_1[1], 0, PACK, QUARTER, HALF)
        weave(vector_copy, quads_1[1], picked_1[1], 2, PACK, 0, QUARTER)
        quantize_x(0, "x_plane_1_0")
        cast_w(scalar_copy, 1, 0, 86, P)
        cast_w(vector_copy, 1, 0, 0, 86)
        cast_w(scalar_copy, 1, 1, 76, P)
        cast_w(vector_copy, 1, 1, 0, 76)
        for t in range(PACK):
            quantize_w(1, t, t + 1)
        quantize_x(1, "w_bf_1_0")

        z_rows = [keep.tile([P, PACK, HALF], BF16, name="z_rows_%d" % a) for a in range(2)]
        z_codes = keep.tile([P, S], U32, name="z_codes", align_bytes=64)
        z_plane = keep.tile([P, S], U8, name="z_plane", align_bytes=64)
        for t, lo, hi, bank in groups:
            if (t, lo) not in banks:
                banks[t, lo] = psum.tile([P, hi - lo], F32, name="h_%d_%d" % (t, lo), tag=bank)
                first_product(banks[t, lo], 0, t, lo, hi, True)
            h = banks[t, lo]
            first_product(h, 1, t, lo, hi, False)
            nc.scalar.activation(out=delayed[:, t, lo + 1 : hi + 1], in_=h[:], func=COPY, scale=tap[:, t, 1:2])
            nc.vector.scalar_tensor_tensor(
                out=z_rows[lo // HALF][:, t, lo % HALF : lo % HALF + hi - lo],
                in0=h[:],
                scalar=tap[:, t, 0:1],
                in1=delayed[:, t, lo:hi],
                op0=MULT,
                op1=ADD,
            )

        z_bf = {}
        for q in range(4):
            z_bf[q] = keep.tile([P, QUARTER * PACK], BF16, name="z_bf_%d" % q, align_bytes=64)

        def weave_z(copy, q, n0=0, n1=QUARTER):
            a, lo = q // 2, (q % 2) * QUARTER
            copy(
                z_bf[q][:].rearrange("p (c i t) -> p c t i", i=4, t=PACK)[:, n0 // 4 : n1 // 4, :, :],
                z_rows[a][:, :, lo + n0 : lo + n1].rearrange("p t (c i) -> p c t i", i=4),
            )

        result = [keep.tile([P, HALF], F32, name="result_%d" % a, align_bytes=1024) for a in range(2)]

        def quantize_z(q):
            lo, hi = q * QUARTER, (q + 1) * QUARTER
            nc.vector.quantize_mx(
                out=z_codes[:, lo:hi].bitcast(FP8X4), scales=z_plane[:, lo:hi], in_=z_bf[q][:]
            )

        def second_product(copy, lo, hi, bank):
            acc = psum.tile([P, hi - lo], F32, name="acc_%d" % lo, tag=bank)
            nc.tensor.matmul_mx(
                out=acc[:],
                lhsT=w2_codes[:].bitcast(FP4X4),
                lhsT_scale=w2_plane[:],
                rhs=z_codes[:, lo:hi].bitcast(FP8X4),
                rhs_scale=z_plane[:, lo:hi],
                start=True,
                stop=True,
            )
            copy(result[lo // HALF][:, lo % HALF : lo % HALF + hi - lo], acc[:])

        nc.gpsimd.tensor_scalar(
            z_bf[0][:].rearrange("p (c i t) -> p c t i", i=4, t=PACK),
            z_rows[0][:, :, 0:QUARTER].rearrange("p t (c i) -> p c t i", i=4),
            1.0,
            0.0,
            MULT,
            ADD,
        )
        weave_z(scalar_move, 1)
        quantize_z(0)
        weave_z(vector_copy, 2, 0, 40)
        weave_z(vector_copy, 3)
        weave_z(scalar_move, 2, 40, QUARTER)
        second_product(scalar_move, 0, QUARTER, "bank_0")
        quantize_z(1)
        second_product(scalar_move, QUARTER, HALF, "bank_4")
        nc.sync.dma_start(out=out[:, 0:HALF], in_=result[0][:])
        quantize_z(3)
        quantize_z(2)
        second_product(vector_copy, 3 * QUARTER, S, "bank_3")
        nc.sync.dma_start(out=out[:, 3 * QUARTER : S], in_=result[1][:, QUARTER:HALF])
        second_product(vector_copy, HALF, 3 * QUARTER, "bank_2")
        nc.sync.dma_start(out=out[:, HALF : 3 * QUARTER], in_=result[1][:, 0:QUARTER])
